import numpy as np
import ml_dtypes


def mxq(x, axis, fmt="e4m3"):
    dtype, down = {"e4m3": (ml_dtypes.float8_e4m3fn, 7), "e5m2": (ml_dtypes.float8_e5m2, 14)}[fmt]
    v = np.moveaxis(np.asarray(x, np.float32).astype(ml_dtypes.bfloat16).astype(np.float64), axis, -1)
    blocks = v.reshape(v.shape[:-1] + (-1, 32))
    amax = np.abs(blocks).max(-1, keepdims=True)
    byte = np.maximum(np.where(amax > 0, np.frexp(amax)[1] - 1 + 127, 0) - down, 1)
    scale = np.exp2(byte - 127.0)
    codes = (blocks / scale).astype(np.float32).astype(dtype).astype(np.float64)
    return np.moveaxis((codes * scale).reshape(v.shape), -1, axis)


WIDE = False


def mx_kscale(k):
    if not WIDE:
        return np.ones(k)
    levels = np.array([10, -10, 5, -5, 0])
    if k % 512:
        return np.exp2(np.random.permutation(np.resize(levels, k // 32))).repeat(32)
    a = np.empty((k // 512, 16))
    for p in range(k // 512):
        a[p, :8] = np.random.permutation(np.resize(levels, 8))
        for g in range(8):
            far = levels[np.abs(levels - a[p, g]) >= 10]
            a[p, g + 8] = far[np.random.randint(len(far))]
    return np.exp2(a.ravel()).repeat(32)


def f64(x):
    return np.asarray(x).astype(np.float64)


def striped(idx):
    return np.tile(idx.reshape(-1, 16).T, (8, 1)).astype(np.uint16)


def unstriped(offs):
    return offs[:16].T.reshape(-1).astype(np.int64)


def pack_weight(w):
    k, n = w.shape
    w = f64(np.asarray(w, np.float32).astype(ml_dtypes.bfloat16)).reshape(k // 32, 32, n)
    amax = np.abs(w).max(1)
    byte = np.clip(np.where(amax > 0, np.frexp(amax)[1] - 1 + 127 - 7, 1), 1, 254)
    scaled = (w * np.exp2(127.0 - byte)[:, None, :]).reshape(k, n).astype(np.float32)
    words = np.ascontiguousarray(scaled.reshape(k // 512, 128, 4, n).transpose(0, 1, 3, 2)).astype(ml_dtypes.float8_e4m3fn).view(np.uint8)
    return words, np.ascontiguousarray(byte.astype(np.uint8).reshape(k // 512, 16, n))


def unpack_weight(words, scales):
    g, p, n, _ = words.shape
    vals = np.ascontiguousarray(words).view(ml_dtypes.float8_e4m3fn).astype(np.float64) * np.repeat(np.exp2(scales.astype(np.float64) - 127.0), 8, axis=1)[..., None]
    return vals.transpose(0, 1, 3, 2).reshape(g * 512, n)


K, T, S, N, U = 512, 2048, 1024, 256, 2048
P = 2 ** 7


def setup_inputs():
    n = np.random.standard_normal
    s = mx_kscale(K)[:, None]
    packed_xT = pack_weight(n((K, T)) * s)
    return {
        "x_words": packed_xT[0],
        "x_scales": packed_xT[1],
        "mem": n((N, U)).astype(np.float32),
        "w1": (n((K, N)) / np.sqrt(K) / s).astype(np.float32),
        "old": np.tile(np.random.uniform(0.5, 0.95, S), (P, 1)).astype(np.float32),
        "new": np.tile(np.random.uniform(0.05, 0.5, S), (P, 1)).astype(np.float32),
        "offs": striped(np.random.permutation(T)[:S]),
        "slot": striped(np.random.permutation(U)[:S]),
    }


def reference(x_words, x_scales, mem, w1, old, new, offs, slot):
    xq = unpack_weight(x_words, x_scales)[:, unstriped(offs)]
    y = np.tanh(mxq(f64(w1), 0, "e4m3").T @ xq)
    out = f64(mem).copy()
    out[:, unstriped(slot)] = f64(mem)[:, unstriped(slot)] * f64(old)[:1] + y * f64(new)[:1]
    return out

@@ -1,0 +1,128 @@
+from contextlib import ExitStack
+
+import concourse.mybir as mybir
+from concourse.masks import make_identity
+
+K, T, S, N, U = 512, 2048, 1024, 256, 2048
+FLOPS = 2 * K * S * N
+
+F32 = mybir.dt.float32
+BF16 = mybir.dt.bfloat16
+I32 = mybir.dt.int32
+U32 = mybir.dt.uint32
+U16 = mybir.dt.uint16
+U8 = mybir.dt.uint8
+FP8X4 = mybir.dt.float8_e4m3fn_x4
+ACT = mybir.ActivationFunctionType
+ALU = mybir.AluOpType
+
+P = 128
+PACK = 4
+CHUNKS = S // P
+HALF = S // 2
+BLOCKS = N // P
+
+
+def tile_picked_ema_tanh_p_kernel(tc, x_words, x_scales, mem, w1, old, new, offs, slot, out):
+    nc = tc.nc
+    with ExitStack() as ctx:
+        lists = ctx.enter_context(tc.tile_pool(name="lists", bufs=1))
+        keep = ctx.enter_context(tc.tile_pool(name="keep", bufs=1))
+        psum = ctx.enter_context(tc.psum_pool(name="psum", bufs=1))
+
+        offs_sb = lists.tile([P, S // 16], U16, name="offs_sb")
+        slot_sb = lists.tile([P, S // 16], U16, name="slot_sb")
+        scale_tab = keep.tile([P, T], U8, name="scale_tab", tag="scales_then_w_code", align_bytes=64)
+        warm_in = keep.tile([P, 1], F32, name="warm_in", tag="zeros_then_words", align_bytes=64)
+        w_raw = keep.tile([P, PACK, N], F32, name="w_raw", tag="w_raw_then_mem", align_bytes=64)
+        w_bf = keep.tile([P, N, PACK], BF16, name="w_bf", align_bytes=64)
+        ident = keep.tile([P, P], F32, name="ident")
+        rows = keep.tile([P, P], F32, name="rows")
+        warm = keep.tile([P, 1], F32, name="warm", tag="warm_then_mem", align_bytes=64)
+
+        nc.vector.memset(scale_tab[:].bitcast(I32), 0)
+        nc.vector.memset(warm_in[:], 0.0)
+        make_identity(nc, ident[:])
+        nc.vector.memset(rows[:], 0.0)
+        nc.scalar.activation(warm[:], warm_in[:], ACT.Tanh)
+
+        nc.sync.dma_start(offs_sb[:], offs)
+        nc.sync.dma_start(slot_sb[:], slot)
+        nc.sync.dma_start(w_raw[:], w1.rearrange("(p j) n -> p j n", j=PACK))
+        for q in range(4):
+            nc.sync.dma_start(scale_tab[32 * q : 32 * q + 4, :].bitcast(I32), x_scales[0, 4 * q : 4 * q + 4, :].bitcast(I32))
+        nc.sync.dma_start(rows[0:CHUNKS, :], old[0:1, :].rearrange("a (c n) -> (a c) n", n=P))
+        nc.sync.dma_start(rows[CHUNKS : 2 * CHUNKS, :], new[0:1, :].rearrange("a (c n) -> (a c) n", n=P))
+        word_tab = keep.tile([P, T], U32, name="word_tab", tag="zeros_then_words", align_bytes=64)
+        nc.sync.dma_start(word_tab[:].bitcast(I32), x_words[0].rearrange("p n t -> p (n t)").bitcast(I32))
+
+        nc.scalar.copy(w_bf[:].rearrange("p (c i) t -> p c t i", i=4), w_raw[:].rearrange("p t (c i) -> p c t i", i=4))
+
+        cols_ps = psum.tile([P, 4, P], F32, name="cols_ps", tag="bank0")
+        nc.tensor.transpose(cols_ps[:, 0, :], rows[:], ident[:])
+        cols = keep.tile([P, 2 * CHUNKS], F32, name="cols")
+        nc.scalar.copy(cols[:], cols_ps[:, 0, 0 : 2 * CHUNKS])
+
+        x_scale = keep.tile([P, S], U8, name="x_scale", align_bytes=64)
+        nc.vector.tensor_copy(x_scale[:], scale_tab[:].indirect(offs_sb[:]))
+
+        w_code = keep.tile([P, N], U32, name="w_code", tag="scales_then_w_code", align_bytes=64)
+        w_scale = keep.tile([P, N], U8, name="w_scale", align_bytes=64)
+        nc.vector.quantize_mx(out=w_code[:].bitcast(FP8X4), scales=w_scale[:], in_=w_bf[:].rearrange("p n t -> p (n t)"))
+
+        mem_sb = []
+        for b, tag in enumerate(("warm_then_mem", "w_raw_then_mem")):
+            mem_sb.append(keep.tile([P, U], F32, name="mem%d" % b, tag=tag, align_bytes=64))
+            nc.sync.dma_start(mem_sb[b][:], mem[b * P : (b + 1) * P, :])
+
+        old_all = keep.tile([P, S], F32, name="old_all")
+        for h in range(2):
+            spread = psum.tile([P, 4, P], F32, name="spread", tag="bank%d" % (h + 1))
+            for i in range(4):
+                c = 4 * h + i
+                nc.tensor.transpose(spread[:, i, :], cols[:, c : c + 1].to_broadcast([P, P]), ident[:])
+            nc.scalar.copy(old_all[:, h * HALF : (h + 1) * HALF], spread[:].rearrange("p i n -> p (i n)"))
+
+        x_word = [keep.tile([P, HALF], U32, name="x_word%d" % h, align_bytes=64) for h in range(2)]
+        for h in range(2):
+            nc.vector.tensor_copy(x_word[h][:], word_tab[:].indirect(offs_sb[:, h * 32 : (h + 1) * 32]))
+
+        fresh = [keep.tile([P, S], F32, name="fresh%d" % b) for b in range(BLOCKS)]
+        for h in range(2):
+            scaled = keep.tile([P, 4, N], F32, name="scaled%d" % h)
+            for pair in range(2):
+                z = psum.tile([P, 2, N], F32, name="z", tag="bank%d" % ((2 * h + pair) % 3))
+                for i in range(2):
+                    lo = (2 * pair + i) * P
+                    nc.tensor.matmul_mx(
+                        out=z[:, i, :],
+                        lhsT=x_word[h][:, lo : lo + P].bitcast(FP8X4),
+                        lhsT_scale=x_scale[:, h * HALF + lo : h * HALF + lo + P],
+                        rhs=w_code[:].bitcast(FP8X4),
+                        rhs_scale=w_scale[:],
+                        start=True,
+                        stop=True,
+                    )
+                y = keep.tile([P, 2, N], F32, name="y%d%d" % (h, pair))
+                nc.scalar.activation(y[:], z[:], ACT.Tanh)
+                for i in range(2):
+                    c = 4 * h + 2 * pair + i
+                    nc.scalar.activation(scaled[:, 2 * pair + i, :], y[:, i, :], ACT.Copy, scale=cols[:, CHUNKS + c : CHUNKS + c + 1])
+            for b in range(BLOCKS):
+                back = psum.tile([P, 4, P], F32, name="back", tag="bank%d" % (4 + 2 * h + b))
+                for i in range(4):
+                    nc.tensor.transpose(back[:, i, :], scaled[:, i, b * P : (b + 1) * P], ident[:])
+                nc.scalar.copy(fresh[b][:, h * HALF : (h + 1) * HALF], back[:].rearrange("p i n -> p (i n)"))
+
+        kept = [keep.tile([P, S], F32, name="kept%d" % b) for b in range(BLOCKS)]
+        for b in range(BLOCKS):
+            nc.vector.tensor_tensor(kept[b][:], mem_sb[b][:].indirect(slot_sb[:]), old_all[:], ALU.mult)
+        for b in range(BLOCKS):
+            pieces = 2 if b == 0 else 1
+            width = S // pieces
+            for h in range(pieces):
+                cols_h = slice(h * width, (h + 1) * width)
+                nc.vector.tensor_tensor(
+                    mem_sb[b][:].indirect(slot_sb[:, h * width // 16 : (h + 1) * width // 16]), kept[b][:, cols_h], fresh[b][:, cols_h], ALU.add
+                )
+            nc.sync.dma_start(out[b * P : (b + 1) * P, :], mem_sb[b][:])

@@ -1,7 +1,6 @@
 from contextlib import ExitStack
 
 import concourse.mybir as mybir
-from concourse.masks import make_identity
 
 K, T, S, N, U = 512, 2048, 1024, 256, 2048
 FLOPS = 2 * K * S * N
@@ -30,99 +29,101 @@ def tile_picked_ema_tanh_p_kernel(tc, x_words, x_scales, mem, w1, old, new, offs
         keep = ctx.enter_context(tc.tile_pool(name="keep", bufs=1))
         psum = ctx.enter_context(tc.psum_pool(name="psum", bufs=1))
 
+        shared = ctx.enter_context(tc.tile_pool(name="shared", bufs=1))
+
         offs_sb = lists.tile([P, S // 16], U16, name="offs_sb")
         slot_sb = lists.tile([P, S // 16], U16, name="slot_sb")
-        scale_tab = keep.tile([P, T], U8, name="scale_tab", tag="scales_then_w_code", align_bytes=64)
-        warm_in = keep.tile([P, 1], F32, name="warm_in", tag="zeros_then_words", align_bytes=64)
-        w_raw = keep.tile([P, PACK, N], F32, name="w_raw", tag="w_raw_then_mem", align_bytes=64)
-        w_bf = keep.tile([P, N, PACK], BF16, name="w_bf", align_bytes=64)
+        scale_tab = keep.tile([P, T], U8, name="scale_tab", tag="scales_then_words", align_bytes=64)
         ident = keep.tile([P, P], F32, name="ident")
-        rows = keep.tile([P, P], F32, name="rows")
-        warm = keep.tile([P, 1], F32, name="warm", tag="warm_then_mem", align_bytes=64)
+        old_cols = keep.tile([P, CHUNKS], F32, name="old_cols")
+        ramp = shared.tile([P, P], I32, name="ramp", offset=7936)
+        new_rows = shared.tile([P, P], F32, name="new_rows", offset=8192)
+        warm = shared.tile([P, 16], F32, name="warm", offset=20448)
+        word_tab = shared.tile([P, T], U32, name="word_tab", offset=0)
+        w_raw = shared.tile([P, PACK, N], F32, name="w_raw", offset=16384)
+        mem_sb = [shared.tile([P, U], F32, name="mem%d" % b, offset=at) for b, at in enumerate((20480, 8192))]
 
         nc.vector.memset(scale_tab[:].bitcast(I32), 0)
-        nc.vector.memset(warm_in[:], 0.0)
-        make_identity(nc, ident[:])
-        nc.vector.memset(rows[:], 0.0)
-        nc.scalar.activation(warm[:], warm_in[:], ACT.Tanh)
+        nc.gpsimd.iota(ramp[:], pattern=[[1, P]], base=0, channel_multiplier=-1)
+        nc.vector.tensor_scalar(ident[:], ramp[:], 0.0, None, ALU.is_equal)
+        nc.vector.memset(new_rows[:], 0.0)
+        nc.scalar.activation(warm[:], ident[:, 0:16], ACT.Tanh)
 
         nc.sync.dma_start(offs_sb[:], offs)
         nc.sync.dma_start(slot_sb[:], slot)
-        nc.sync.dma_start(w_raw[:], w1.rearrange("(p j) n -> p j n", j=PACK))
+        nc.sync.dma_start(old_cols[:], old[0:1, :].rearrange("a (n e) -> (a n) e", e=CHUNKS))
         for q in range(4):
             nc.sync.dma_start(scale_tab[32 * q : 32 * q + 4, :].bitcast(I32), x_scales[0, 4 * q : 4 * q + 4, :].bitcast(I32))
-        nc.sync.dma_start(rows[0:CHUNKS, :], old[0:1, :].rearrange("a (c n) -> (a c) n", n=P))
-        nc.sync.dma_start(rows[CHUNKS : 2 * CHUNKS, :], new[0:1, :].rearrange("a (c n) -> (a c) n", n=P))
-        word_tab = keep.tile([P, T], U32, name="word_tab", tag="zeros_then_words", align_bytes=64)
         nc.sync.dma_start(word_tab[:].bitcast(I32), x_words[0].rearrange("p n t -> p (n t)").bitcast(I32))
-
-        nc.scalar.copy(w_bf[:].rearrange("p (c i) t -> p c t i", i=4), w_raw[:].rearrange("p t (c i) -> p c t i", i=4))
-
-        cols_ps = psum.tile([P, 4, P], F32, name="cols_ps", tag="bank0")
-        nc.tensor.transpose(cols_ps[:, 0, :], rows[:], ident[:])
-        cols = keep.tile([P, 2 * CHUNKS], F32, name="cols")
-        nc.scalar.copy(cols[:], cols_ps[:, 0, 0 : 2 * CHUNKS])
-
-        x_scale = keep.tile([P, S], U8, name="x_scale", align_bytes=64)
-        nc.vector.tensor_copy(x_scale[:], scale_tab[:].indirect(offs_sb[:]))
-
-        w_code = keep.tile([P, N], U32, name="w_code", tag="scales_then_w_code", align_bytes=64)
-        w_scale = keep.tile([P, N], U8, name="w_scale", align_bytes=64)
-        nc.vector.quantize_mx(out=w_code[:].bitcast(FP8X4), scales=w_scale[:], in_=w_bf[:].rearrange("p n t -> p (n t)"))
-
-        mem_sb = []
-        for b, tag in enumerate(("warm_then_mem", "w_raw_then_mem")):
-            mem_sb.append(keep.tile([P, U], F32, name="mem%d" % b, tag=tag, align_bytes=64))
-            nc.sync.dma_start(mem_sb[b][:], mem[b * P : (b + 1) * P, :])
+        nc.sync.dma_start(new_rows[0:CHUNKS, :], new[0:1, :].rearrange("a (c n) -> (a c) n", n=P))
+        nc.sync.dma_start(w_raw[:], w1.rearrange("(p j) n -> p j n", j=PACK))
+        nc.sync.dma_start(mem_sb[0][:], mem[0:P, :])
 
         old_all = keep.tile([P, S], F32, name="old_all")
         for h in range(2):
             spread = psum.tile([P, 4, P], F32, name="spread", tag="bank%d" % (h + 1))
             for i in range(4):
-                c = 4 * h + i
-                nc.tensor.transpose(spread[:, i, :], cols[:, c : c + 1].to_broadcast([P, P]), ident[:])
-            nc.scalar.copy(old_all[:, h * HALF : (h + 1) * HALF], spread[:].rearrange("p i n -> p (i n)"))
+                e = 4 * h + i
+                nc.tensor.transpose(spread[:, i, :], old_cols[:, e : e + 1].to_broadcast([P, P]), ident[:])
+            nc.scalar.copy(old_all[:].rearrange("p (n e) -> p n e", e=CHUNKS)[:, :, 4 * h : 4 * h + 4], spread[:].rearrange("p i n -> p n i"))
 
-        x_word = [keep.tile([P, HALF], U32, name="x_word%d" % h, align_bytes=64) for h in range(2)]
-        for h in range(2):
-            nc.vector.tensor_copy(x_word[h][:], word_tab[:].indirect(offs_sb[:, h * 32 : (h + 1) * 32]))
+        cols_ps = psum.tile([P, 4, P], F32, name="cols_ps", tag="bank0")
+        nc.tensor.transpose(cols_ps[:, 0, :], new_rows[:], ident[:])
+        new_cols = keep.tile([P, CHUNKS], F32, name="new_cols")
+        nc.scalar.copy(new_cols[:], cols_ps[:, 0, 0:CHUNKS])
+        nc.sync.dma_start(mem_sb[1][:], mem[P : 2 * P, :])
 
-        fresh = [keep.tile([P, S], F32, name="fresh%d" % b) for b in range(BLOCKS)]
+        x_scale = keep.tile([P, S], U8, name="x_scale", align_bytes=64)
+        nc.vector.tensor_copy(x_scale[:], scale_tab[:].indirect(offs_sb[:]))
+        x_word = keep.tile([P, S], U32, name="x_word", tag="scales_then_words", align_bytes=64)
+        nc.vector.tensor_copy(x_word[:], word_tab[:].indirect(offs_sb[:]))
+
+        w_bf = keep.tile([P, N, PACK], BF16, name="w_bf", align_bytes=64)
+        nc.scalar.copy(w_bf[:].rearrange("p (c i) t -> p c t i", i=4), w_raw[:].rearrange("p t (c i) -> p c t i", i=4))
+        w_code = keep.tile([P, N], U32, name="w_code", align_bytes=64)
+        w_scale = keep.tile([P, N], U8, name="w_scale", align_bytes=64)
+        nc.vector.quantize_mx(out=w_code[:].bitcast(FP8X4), scales=w_scale[:], in_=w_bf[:].rearrange("p n t -> p (n t)"))
+
+        scaled = [keep.tile([P, 4, N], F32, name="scaled%d" % h) for h in range(2)]
+        fresh_first = [keep.tile([P, HALF], F32, name="fresh_first%d" % h) for h in range(2)]
+        fresh_last = keep.tile([P, S], F32, name="fresh_last")
+        z_banks = ((0, 1), (4, 2))
+
+        def turn_back(h, b, target):
+            back = psum.tile([P, 4, P], F32, name="back", tag="bank%d" % (4 + 2 * h + b))
+            for i in range(4):
+                nc.tensor.transpose(back[:, i, :], scaled[h][:, i, b * P : (b + 1) * P], ident[:])
+            nc.scalar.copy(target, back[:].rearrange("p i n -> p (i n)"))
+
         for h in range(2):
-            scaled = keep.tile([P, 4, N], F32, name="scaled%d" % h)
+            y = keep.tile([P, 4, N], F32, name="y%d" % h)
             for pair in range(2):
-                z = psum.tile([P, 2, N], F32, name="z", tag="bank%d" % ((2 * h + pair) % 3))
+                z = psum.tile([P, 2, N], F32, name="z", tag="bank%d" % z_banks[h][pair])
                 for i in range(2):
-                    lo = (2 * pair + i) * P
+                    lo = (4 * h + 2 * pair + i) * P
                     nc.tensor.matmul_mx(
                         out=z[:, i, :],
-                        lhsT=x_word[h][:, lo : lo + P].bitcast(FP8X4),
-                        lhsT_scale=x_scale[:, h * HALF + lo : h * HALF + lo + P],
+                        lhsT=x_word[:, lo : lo + P].bitcast(FP8X4),
+                        lhsT_scale=x_scale[:, lo : lo + P],
                         rhs=w_code[:].bitcast(FP8X4),
                         rhs_scale=w_scale[:],
                         start=True,
                         stop=True,
                     )
-                y = keep.tile([P, 2, N], F32, name="y%d%d" % (h, pair))
-                nc.scalar.activation(y[:], z[:], ACT.Tanh)
-                for i in range(2):
-                    c = 4 * h + 2 * pair + i
-                    nc.scalar.activation(scaled[:, 2 * pair + i, :], y[:, i, :], ACT.Copy, scale=cols[:, CHUNKS + c : CHUNKS + c + 1])
-            for b in range(BLOCKS):
-                back = psum.tile([P, 4, P], F32, name="back", tag="bank%d" % (4 + 2 * h + b))
-                for i in range(4):
-                    nc.tensor.transpose(back[:, i, :], scaled[:, i, b * P : (b + 1) * P], ident[:])
-                nc.scalar.copy(fresh[b][:, h * HALF : (h + 1) * HALF], back[:].rearrange("p i n -> p (i n)"))
+                nc.scalar.activation(y[:, 2 * pair : 2 * pair + 2, :], z[:], ACT.Tanh)
+            for i in range(4):
+                c = 4 * h + i
+                nc.scalar.activation(scaled[h][:, i, :], y[:, i, :], ACT.Copy, scale=new_cols[:, c : c + 1])
+            turn_back(h, 0, fresh_first[h][:])
+        for h in range(2):
+            turn_back(h, 1, fresh_last[:, h * HALF : (h + 1) * HALF])
 
         kept = [keep.tile([P, S], F32, name="kept%d" % b) for b in range(BLOCKS)]
         for b in range(BLOCKS):
             nc.vector.tensor_tensor(kept[b][:], mem_sb[b][:].indirect(slot_sb[:]), old_all[:], ALU.mult)
-        for b in range(BLOCKS):
-            pieces = 2 if b == 0 else 1
-            width = S // pieces
-            for h in range(pieces):
-                cols_h = slice(h * width, (h + 1) * width)
-                nc.vector.tensor_tensor(
-                    mem_sb[b][:].indirect(slot_sb[:, h * width // 16 : (h + 1) * width // 16]), kept[b][:, cols_h], fresh[b][:, cols_h], ALU.add
-                )
-            nc.sync.dma_start(out[b * P : (b + 1) * P, :], mem_sb[b][:])
+        for h in range(2):
+            window = mem_sb[0][:].indirect(slot_sb[:, h * 32 : (h + 1) * 32])
+            nc.vector.tensor_tensor(window, kept[0][:, h * HALF : (h + 1) * HALF], fresh_first[h][:], ALU.add)
+        nc.sync.dma_start(out[0:P, :], mem_sb[0][:])
+        nc.vector.tensor_tensor(mem_sb[1][:].indirect(slot_sb[:]), kept[1][:], fresh_last[:], ALU.add)
+        nc.sync.dma_start(out[P : 2 * P, :], mem_sb[1][:])

@@ -37,25 +37,26 @@ def tile_picked_ema_tanh_p_kernel(tc, x_words, x_scales, mem, w1, old, new, offs
         ident = keep.tile([P, P], F32, name="ident")
         old_cols = keep.tile([P, CHUNKS], F32, name="old_cols")
         ramp = shared.tile([P, P], I32, name="ramp", offset=7936)
-        new_rows = shared.tile([P, P], F32, name="new_rows", offset=8192)
-        warm = shared.tile([P, 16], F32, name="warm", offset=20448)
+        new_rows = shared.tile([P, P], F32, name="new_rows", offset=9216)
+        warm = shared.tile([P, 16], F32, name="warm", offset=21472)
         word_tab = shared.tile([P, T], U32, name="word_tab", offset=0)
-        w_raw = shared.tile([P, PACK, N], F32, name="w_raw", offset=16384)
-        mem_sb = [shared.tile([P, U], F32, name="mem%d" % b, offset=at) for b, at in enumerate((20480, 8192))]
+        w_raw = shared.tile([P, PACK, N], F32, name="w_raw", offset=17408)
+        mem_sb = [shared.tile([P, U], F32, name="mem%d" % b, offset=at) for b, at in enumerate((21504, 9216))]
 
         nc.vector.memset(scale_tab[:].bitcast(I32), 0)
         nc.gpsimd.iota(ramp[:], pattern=[[1, P]], base=0, channel_multiplier=-1)
         nc.vector.tensor_scalar(ident[:], ramp[:], 0.0, None, ALU.is_equal)
-        nc.vector.memset(new_rows[:], 0.0)
+        nc.gpsimd.memset(new_rows[:], 0.0)
         nc.scalar.activation(warm[:], ident[:, 0:16], ACT.Tanh)
 
         nc.sync.dma_start(offs_sb[:], offs)
         nc.sync.dma_start(slot_sb[:], slot)
-        nc.sync.dma_start(old_cols[:], old[0:1, :].rearrange("a (n e) -> (a n) e", e=CHUNKS))
+        nc.scalar.dma_start(old_cols[:], old[0:1, :].rearrange("a (n e) -> (a n) e", e=CHUNKS))
         for q in range(4):
-            nc.sync.dma_start(scale_tab[32 * q : 32 * q + 4, :].bitcast(I32), x_scales[0, 4 * q : 4 * q + 4, :].bitcast(I32))
+            queue = nc.sync if q < 2 else nc.scalar
+            queue.dma_start(scale_tab[32 * q : 32 * q + 4, :].bitcast(I32), x_scales[0, 4 * q : 4 * q + 4, :].bitcast(I32))
         nc.sync.dma_start(word_tab[:].bitcast(I32), x_words[0].rearrange("p n t -> p (n t)").bitcast(I32))
-        nc.sync.dma_start(new_rows[0:CHUNKS, :], new[0:1, :].rearrange("a (c n) -> (a c) n", n=P))
+        nc.gpsimd.dma_start(new_rows[0:CHUNKS, :], new[0:1, :].rearrange("a (c n) -> (a c) n", n=P))
         nc.sync.dma_start(w_raw[:], w1.rearrange("(p j) n -> p j n", j=PACK))
         nc.sync.dma_start(mem_sb[0][:], mem[0:P, :])
 
@@ -73,7 +74,7 @@ def tile_picked_ema_tanh_p_kernel(tc, x_words, x_scales, mem, w1, old, new, offs
         nc.scalar.copy(new_cols[:], cols_ps[:, 0, 0:CHUNKS])
         nc.sync.dma_start(mem_sb[1][:], mem[P : 2 * P, :])
 
-        x_scale = keep.tile([P, S], U8, name="x_scale", align_bytes=64)
+        x_scale = shared.tile([P, S], U8, name="x_scale", offset=8192, align_bytes=64)
         nc.vector.tensor_copy(x_scale[:], scale_tab[:].indirect(offs_sb[:]))
         x_word = keep.tile([P, S], U32, name="x_word", tag="scales_then_words", align_bytes=64)
         nc.vector.tensor_copy(x_word[:], word_tab[:].indirect(offs_sb[:]))

@@ -29,38 +29,37 @@ def tile_picked_ema_tanh_p_kernel(tc, x_words, x_scales, mem, w1, old, new, offs
         keep = ctx.enter_context(tc.tile_pool(name="keep", bufs=1))
         psum = ctx.enter_context(tc.psum_pool(name="psum", bufs=1))
 
-        shared = ctx.enter_context(tc.tile_pool(name="shared", bufs=1))
 
         offs_sb = lists.tile([P, S // 16], U16, name="offs_sb")
         slot_sb = lists.tile([P, S // 16], U16, name="slot_sb")
-        scale_tab = keep.tile([P, T], U8, name="scale_tab", tag="scales_then_words", align_bytes=64)
+        shared = ctx.enter_context(tc.tile_pool(name="shared", bufs=1))
+        scale_tab = shared.tile([P, T], U8, name="scale_tab", offset=3072)
         ident = keep.tile([P, P], F32, name="ident")
         old_cols = keep.tile([P, CHUNKS], F32, name="old_cols")
-        ramp = shared.tile([P, P], I32, name="ramp", offset=7936)
-        new_rows = shared.tile([P, P], F32, name="new_rows", offset=9216)
-        warm = shared.tile([P, 16], F32, name="warm", offset=21472)
-        word_tab = shared.tile([P, T], U32, name="word_tab", offset=0)
-        w_raw = shared.tile([P, PACK, N], F32, name="w_raw", offset=17408)
-        mem_sb = [shared.tile([P, U], F32, name="mem%d" % b, offset=at) for b, at in enumerate((21504, 9216))]
+        ramp = keep.tile([P, P], I32, name="ramp", tag="ramp_then_scales", align_bytes=64)
+        new_rows = keep.tile([P, P], F32, name="new_rows")
+        word_tab = keep.tile([P, T], U32, name="word_tab", tag="words_then_codes", align_bytes=64)
+        w_raw = keep.tile([P, PACK, N], F32, name="w_raw")
+        mem_sb = [keep.tile([P, U], F32, name="mem0"), shared.tile([P, U], F32, name="mem1", offset=4096)]
 
-        nc.vector.memset(scale_tab[:].bitcast(I32), 0)
+        for lo, hi in ((0, 16), (32, 64), (64, P)):
+            nc.vector.memset(scale_tab[lo:hi, :].bitcast(I32), 0)
+        x_plane = keep.tile([P, S], U8, name="x_plane", align_bytes=64)
+        nc.gpsimd.memset(x_plane[:].bitcast(I32), 0)
         nc.gpsimd.iota(ramp[:], pattern=[[1, P]], base=0, channel_multiplier=-1)
+        nc.vector.memset(new_rows[:], 0.0)
         nc.vector.tensor_scalar(ident[:], ramp[:], 0.0, None, ALU.is_equal)
-        nc.gpsimd.memset(new_rows[:], 0.0)
-        nc.scalar.activation(warm[:], ident[:, 0:16], ACT.Tanh)
 
         nc.sync.dma_start(offs_sb[:], offs)
-        nc.sync.dma_start(slot_sb[:], slot)
         nc.scalar.dma_start(old_cols[:], old[0:1, :].rearrange("a (n e) -> (a n) e", e=CHUNKS))
-        for q in range(4):
-            queue = nc.sync if q < 2 else nc.scalar
-            queue.dma_start(scale_tab[32 * q : 32 * q + 4, :].bitcast(I32), x_scales[0, 4 * q : 4 * q + 4, :].bitcast(I32))
+        nc.sync.dma_start(scale_tab[16:32, :].bitcast(I32), x_scales[0].bitcast(I32))
         nc.sync.dma_start(word_tab[:].bitcast(I32), x_words[0].rearrange("p n t -> p (n t)").bitcast(I32))
-        nc.gpsimd.dma_start(new_rows[0:CHUNKS, :], new[0:1, :].rearrange("a (c n) -> (a c) n", n=P))
         nc.sync.dma_start(w_raw[:], w1.rearrange("(p j) n -> p j n", j=PACK))
+        nc.sync.dma_start(slot_sb[:], slot)
+        nc.sync.dma_start(new_rows[0:CHUNKS, :], new[0:1, :].rearrange("a (c n) -> (a c) n", n=P))
         nc.sync.dma_start(mem_sb[0][:], mem[0:P, :])
 
-        old_all = keep.tile([P, S], F32, name="old_all")
+        old_all = keep.tile([P, S], F32, name="old_all", tag="old_then_fresh")
         for h in range(2):
             spread = psum.tile([P, 4, P], F32, name="spread", tag="bank%d" % (h + 1))
             for i in range(4):
@@ -72,59 +71,57 @@ def tile_picked_ema_tanh_p_kernel(tc, x_words, x_scales, mem, w1, old, new, offs
         nc.tensor.transpose(cols_ps[:, 0, :], new_rows[:], ident[:])
         new_cols = keep.tile([P, CHUNKS], F32, name="new_cols")
         nc.scalar.copy(new_cols[:], cols_ps[:, 0, 0:CHUNKS])
-        nc.sync.dma_start(mem_sb[1][:], mem[P : 2 * P, :])
 
-        x_scale = shared.tile([P, S], U8, name="x_scale", offset=8192, align_bytes=64)
+        x_scale = keep.tile([P, S], U8, name="x_scale", tag="ramp_then_scales", align_bytes=64)
         nc.vector.tensor_copy(x_scale[:], scale_tab[:].indirect(offs_sb[:]))
-        x_word = keep.tile([P, S], U32, name="x_word", tag="scales_then_words", align_bytes=64)
+        for q in range(4):
+            nc.sync.dma_start(x_plane[32 * q : 32 * q + 4, :].bitcast(I32), x_scale[16 + 4 * q : 20 + 4 * q, :].bitcast(I32))
+        nc.sync.dma_start(mem_sb[1][:], mem[P : 2 * P, :])
+        x_word = shared.tile([P, S], U32, name="x_word", offset=0, align_bytes=64)
         nc.vector.tensor_copy(x_word[:], word_tab[:].indirect(offs_sb[:]))
 
         w_bf = keep.tile([P, N, PACK], BF16, name="w_bf", align_bytes=64)
         nc.scalar.copy(w_bf[:].rearrange("p (c i) t -> p c t i", i=4), w_raw[:].rearrange("p t (c i) -> p c t i", i=4))
-        w_code = keep.tile([P, N], U32, name="w_code", align_bytes=64)
+        w_code = keep.tile([P, N], U32, name="w_code", tag="words_then_codes", align_bytes=64)
         w_scale = keep.tile([P, N], U8, name="w_scale", align_bytes=64)
         nc.vector.quantize_mx(out=w_code[:].bitcast(FP8X4), scales=w_scale[:], in_=w_bf[:].rearrange("p n t -> p (n t)"))
 
-        scaled = [keep.tile([P, 4, N], F32, name="scaled%d" % h) for h in range(2)]
-        fresh_first = [keep.tile([P, HALF], F32, name="fresh_first%d" % h) for h in range(2)]
-        fresh_last = keep.tile([P, S], F32, name="fresh_last")
-        z_banks = ((0, 1), (4, 2))
-
-        def turn_back(h, b, target):
-            back = psum.tile([P, 4, P], F32, name="back", tag="bank%d" % (4 + 2 * h + b))
+        def fresh_half(b, h, target):
+            z = psum.tile([P, 4, P], F32, name="z", tag="bank%d" % (3 + h))
             for i in range(4):
-                nc.tensor.transpose(back[:, i, :], scaled[h][:, i, b * P : (b + 1) * P], ident[:])
-            nc.scalar.copy(target, back[:].rearrange("p i n -> p (i n)"))
-
-        for h in range(2):
-            y = keep.tile([P, 4, N], F32, name="y%d" % h)
-            for pair in range(2):
-                z = psum.tile([P, 2, N], F32, name="z", tag="bank%d" % z_banks[h][pair])
-                for i in range(2):
-                    lo = (4 * h + 2 * pair + i) * P
-                    nc.tensor.matmul_mx(
-                        out=z[:, i, :],
-                        lhsT=x_word[:, lo : lo + P].bitcast(FP8X4),
-                        lhsT_scale=x_scale[:, lo : lo + P],
-                        rhs=w_code[:].bitcast(FP8X4),
-                        rhs_scale=w_scale[:],
-                        start=True,
-                        stop=True,
-                    )
-                nc.scalar.activation(y[:, 2 * pair : 2 * pair + 2, :], z[:], ACT.Tanh)
+                lo = (4 * h + i) * P
+                nc.tensor.matmul_mx(
+                    out=z[:, i, :],
+                    lhsT=x_word[:, lo : lo + P].bitcast(FP8X4),
+                    lhsT_scale=x_plane[:, lo : lo + P],
+                    rhs=w_code[:, b * P : (b + 1) * P].bitcast(FP8X4),
+                    rhs_scale=w_scale[:, b * P : (b + 1) * P],
+                    start=True,
+                    stop=True,
+                )
+            y = keep.tile([P, 4, P], F32, name="y%d%d" % (b, h))
+            nc.scalar.activation(y[:], z[:], ACT.Tanh)
+            scaled = keep.tile([P, 4, P], F32, name="scaled%d%d" % (b, h))
+            back = psum.tile([P, 4, P], F32, name="back", tag="bank%d" % (5 + h))
             for i in range(4):
                 c = 4 * h + i
-                nc.scalar.activation(scaled[h][:, i, :], y[:, i, :], ACT.Copy, scale=new_cols[:, c : c + 1])
-            turn_back(h, 0, fresh_first[h][:])
+                nc.scalar.activation(scaled[:, i, :], y[:, i, :], ACT.Copy, scale=new_cols[:, c : c + 1])
+                nc.tensor.transpose(back[:, i, :], scaled[:, i, :], ident[:])
+            nc.scalar.copy(target, back[:].rearrange("p i n -> p (i n)"))
+
+        fresh_first = [keep.tile([P, HALF], F32, name="fresh_first%d" % h) for h in range(2)]
         for h in range(2):
-            turn_back(h, 1, fresh_last[:, h * HALF : (h + 1) * HALF])
+            fresh_half(1, h, fresh_first[h][:])
 
         kept = [keep.tile([P, S], F32, name="kept%d" % b) for b in range(BLOCKS)]
         for b in range(BLOCKS):
             nc.vector.tensor_tensor(kept[b][:], mem_sb[b][:].indirect(slot_sb[:]), old_all[:], ALU.mult)
+        fresh_last = keep.tile([P, S], F32, name="fresh_last", tag="old_then_fresh")
         for h in range(2):
-            window = mem_sb[0][:].indirect(slot_sb[:, h * 32 : (h + 1) * 32])
-            nc.vector.tensor_tensor(window, kept[0][:, h * HALF : (h + 1) * HALF], fresh_first[h][:], ALU.add)
-        nc.sync.dma_start(out[0:P, :], mem_sb[0][:])
-        nc.vector.tensor_tensor(mem_sb[1][:].indirect(slot_sb[:]), kept[1][:], fresh_last[:], ALU.add)
+            fresh_half(0, h, fresh_last[:, h * HALF : (h + 1) * HALF])
+        for h in range(2):
+            window = mem_sb[1][:].indirect(slot_sb[:, h * 32 : (h + 1) * 32])
+            nc.vector.tensor_tensor(window, kept[1][:, h * HALF : (h + 1) * HALF], fresh_first[h][:], ALU.add)
         nc.sync.dma_start(out[P : 2 * P, :], mem_sb[1][:])
+        nc.vector.tensor_tensor(mem_sb[0][:].indirect(slot_sb[:]), kept[0][:], fresh_last[:], ALU.add)
+        nc.sync.dma_start(out[0:P, :], mem_sb[0][:])

@@ -1,6 +1,7 @@
 from contextlib import ExitStack
 
 import concourse.mybir as mybir
+from concourse.masks import make_identity
 
 K, T, S, N, U = 512, 2048, 1024, 256, 2048
 FLOPS = 2 * K * S * N
@@ -35,28 +36,25 @@ def tile_picked_ema_tanh_p_kernel(tc, x_words, x_scales, mem, w1, old, new, offs
         shared = ctx.enter_context(tc.tile_pool(name="shared", bufs=1))
         scale_tab = shared.tile([P, T], U8, name="scale_tab", offset=3072)
         ident = keep.tile([P, P], F32, name="ident")
-        old_cols = keep.tile([P, CHUNKS], F32, name="old_cols")
-        ramp = keep.tile([P, P], I32, name="ramp", tag="ramp_then_scales", align_bytes=64)
+        old_cols = keep.tile([P, CHUNKS], F32, name="old_cols", tag="w_bf", align_bytes=64)
         new_rows = keep.tile([P, P], F32, name="new_rows")
         word_tab = keep.tile([P, T], U32, name="word_tab", tag="words_then_codes", align_bytes=64)
         w_raw = keep.tile([P, PACK, N], F32, name="w_raw")
         mem_sb = [keep.tile([P, U], F32, name="mem0"), shared.tile([P, U], F32, name="mem1", offset=4096)]
 
-        for lo, hi in ((0, 16), (32, 64), (64, P)):
-            nc.vector.memset(scale_tab[lo:hi, :].bitcast(I32), 0)
-        x_plane = keep.tile([P, S], U8, name="x_plane", align_bytes=64)
-        nc.gpsimd.memset(x_plane[:].bitcast(I32), 0)
-        nc.gpsimd.iota(ramp[:], pattern=[[1, P]], base=0, channel_multiplier=-1)
         nc.vector.memset(new_rows[:], 0.0)
-        nc.vector.tensor_scalar(ident[:], ramp[:], 0.0, None, ALU.is_equal)
+        nc.vector.memset(scale_tab[0:112, :].bitcast(I32), 0)
+        x_plane = keep.tile([P, S], U8, name="x_plane", align_bytes=64)
+        make_identity(nc, ident[:])
+        nc.vector.memset(x_plane[:].bitcast(I32), 0)
 
         nc.sync.dma_start(offs_sb[:], offs)
         nc.scalar.dma_start(old_cols[:], old[0:1, :].rearrange("a (n e) -> (a n) e", e=CHUNKS))
-        nc.sync.dma_start(scale_tab[16:32, :].bitcast(I32), x_scales[0].bitcast(I32))
+        nc.scalar.dma_start(new_rows[0:CHUNKS, :], new[0:1, :].rearrange("a (c n) -> (a c) n", n=P))
+        nc.sync.dma_start(scale_tab[112:P, :].bitcast(I32), x_scales[0].bitcast(I32))
         nc.sync.dma_start(word_tab[:].bitcast(I32), x_words[0].rearrange("p n t -> p (n t)").bitcast(I32))
         nc.sync.dma_start(w_raw[:], w1.rearrange("(p j) n -> p j n", j=PACK))
         nc.sync.dma_start(slot_sb[:], slot)
-        nc.sync.dma_start(new_rows[0:CHUNKS, :], new[0:1, :].rearrange("a (c n) -> (a c) n", n=P))
         nc.sync.dma_start(mem_sb[0][:], mem[0:P, :])
 
         old_all = keep.tile([P, S], F32, name="old_all", tag="old_then_fresh")
@@ -72,10 +70,10 @@ def tile_picked_ema_tanh_p_kernel(tc, x_words, x_scales, mem, w1, old, new, offs
         new_cols = keep.tile([P, CHUNKS], F32, name="new_cols")
         nc.scalar.copy(new_cols[:], cols_ps[:, 0, 0:CHUNKS])
 
-        x_scale = keep.tile([P, S], U8, name="x_scale", tag="ramp_then_scales", align_bytes=64)
+        x_scale = keep.tile([P, S], U8, name="x_scale")
         nc.vector.tensor_copy(x_scale[:], scale_tab[:].indirect(offs_sb[:]))
         for q in range(4):
-            nc.sync.dma_start(x_plane[32 * q : 32 * q + 4, :].bitcast(I32), x_scale[16 + 4 * q : 20 + 4 * q, :].bitcast(I32))
+            nc.sync.dma_start(x_plane[32 * q : 32 * q + 4, :].bitcast(I32), x_scale[112 + 4 * q : 116 + 4 * q, :].bitcast(I32))
         nc.sync.dma_start(mem_sb[1][:], mem[P : 2 * P, :])
         x_word = shared.tile([P, S], U32, name="x_word", offset=0, align_bytes=64)
         nc.vector.tensor_copy(x_word[:], word_tab[:].indirect(offs_sb[:]))
@@ -87,7 +85,7 @@ def tile_picked_ema_tanh_p_kernel(tc, x_words, x_scales, mem, w1, old, new, offs
         nc.vector.quantize_mx(out=w_code[:].bitcast(FP8X4), scales=w_scale[:], in_=w_bf[:].rearrange("p n t -> p (n t)"))
 
         def fresh_half(b, h, target):
-            z = psum.tile([P, 4, P], F32, name="z", tag="bank%d" % (3 + h))
+            z = psum.tile([P, 4, P], F32, name="z", tag="bank%d" % (1 + h))
             for i in range(4):
                 lo = (4 * h + i) * P
                 nc.tensor.matmul_mx(
@@ -113,7 +111,7 @@ def tile_picked_ema_tanh_p_kernel(tc, x_words, x_scales, mem, w1, old, new, offs
         for h in range(2):
             fresh_half(1, h, fresh_first[h][:])
 
-        kept = [keep.tile([P, S], F32, name="kept%d" % b) for b in range(BLOCKS)]
+        kept = [keep.tile([P, S], F32, name="kept0", tag="w_bf", align_bytes=64), keep.tile([P, S], F32, name="kept1", tag="w_raw")]
         for b in range(BLOCKS):
             nc.vector.tensor_tensor(kept[b][:], mem_sb[b][:].indirect(slot_sb[:]), old_all[:], ALU.mult)
         fresh_last = keep.tile([P, S], F32, name="fresh_last", tag="old_then_fresh")

@@ -57,7 +57,7 @@ def tile_picked_ema_tanh_p_kernel(tc, x_words, x_scales, mem, w1, old, new, offs
         nc.sync.dma_start(slot_sb[:], slot)
         nc.sync.dma_start(mem_sb[0][:], mem[0:P, :])
 
-        old_all = keep.tile([P, S], F32, name="old_all", tag="old_then_fresh")
+        old_all = keep.tile([P, S], F32, name="old_all")
         for h in range(2):
             spread = psum.tile([P, 4, P], F32, name="spread", tag="bank%d" % (h + 1))
             for i in range(4):
@@ -107,19 +107,12 @@ def tile_picked_ema_tanh_p_kernel(tc, x_words, x_scales, mem, w1, old, new, offs
                 nc.tensor.transpose(back[:, i, :], scaled[:, i, :], ident[:])
             nc.scalar.copy(target, back[:].rearrange("p i n -> p (i n)"))
 
-        fresh_first = [keep.tile([P, HALF], F32, name="fresh_first%d" % h) for h in range(2)]
-        for h in range(2):
-            fresh_half(1, h, fresh_first[h][:])
-
         kept = [keep.tile([P, S], F32, name="kept0", tag="w_bf", align_bytes=64), keep.tile([P, S], F32, name="kept1", tag="w_raw")]
         for b in range(BLOCKS):
             nc.vector.tensor_tensor(kept[b][:], mem_sb[b][:].indirect(slot_sb[:]), old_all[:], ALU.mult)
-        fresh_last = keep.tile([P, S], F32, name="fresh_last", tag="old_then_fresh")
-        for h in range(2):
-            fresh_half(0, h, fresh_last[:, h * HALF : (h + 1) * HALF])
-        for h in range(2):
-            window = mem_sb[1][:].indirect(slot_sb[:, h * 32 : (h + 1) * 32])
-            nc.vector.tensor_tensor(window, kept[1][:, h * HALF : (h + 1) * HALF], fresh_first[h][:], ALU.add)
-        nc.sync.dma_start(out[P : 2 * P, :], mem_sb[1][:])
-        nc.vector.tensor_tensor(mem_sb[0][:].indirect(slot_sb[:]), kept[0][:], fresh_last[:], ALU.add)
-        nc.sync.dma_start(out[0:P, :], mem_sb[0][:])
+        for b in range(BLOCKS):
+            fresh = keep.tile([P, S], F32, name="fresh%d" % b)
+            for h in range(2):
+                fresh_half(b, h, fresh[:, h * HALF : (h + 1) * HALF])
+            nc.vector.tensor_tensor(mem_sb[b][:].indirect(slot_sb[:]), kept[b][:], fresh[:], ALU.add)
+            nc.sync.dma_start(out[b * P : (b + 1) * P, :], mem_sb[b][:])

@@ -38,8 +38,8 @@ def tile_picked_ema_tanh_p_kernel(tc, x_words, x_scales, mem, w1, old, new, offs
         ident = keep.tile([P, P], F32, name="ident")
         old_cols = keep.tile([P, CHUNKS], F32, name="old_cols", tag="w_bf", align_bytes=64)
         new_rows = keep.tile([P, P], F32, name="new_rows")
-        word_tab = keep.tile([P, T], U32, name="word_tab", tag="words_then_codes", align_bytes=64)
-        w_raw = keep.tile([P, PACK, N], F32, name="w_raw")
+        word_tab = keep.tile([P, T], U32, name="word_tab")
+        w_raw = shared.tile([P, PACK, N], F32, name="w_raw", offset=14336)
         mem_sb = [keep.tile([P, U], F32, name="mem0"), shared.tile([P, U], F32, name="mem1", offset=4096)]
 
         nc.vector.memset(new_rows[:], 0.0)
@@ -75,12 +75,12 @@ def tile_picked_ema_tanh_p_kernel(tc, x_words, x_scales, mem, w1, old, new, offs
         for q in range(4):
             nc.sync.dma_start(x_plane[32 * q : 32 * q + 4, :].bitcast(I32), x_scale[112 + 4 * q : 116 + 4 * q, :].bitcast(I32))
         nc.sync.dma_start(mem_sb[1][:], mem[P : 2 * P, :])
-        x_word = shared.tile([P, S], U32, name="x_word", offset=0, align_bytes=64)
+        x_word = keep.tile([P, S], U32, name="x_word", align_bytes=64)
         nc.vector.tensor_copy(x_word[:], word_tab[:].indirect(offs_sb[:]))
 
         w_bf = keep.tile([P, N, PACK], BF16, name="w_bf", align_bytes=64)
         nc.scalar.copy(w_bf[:].rearrange("p (c i) t -> p c t i", i=4), w_raw[:].rearrange("p t (c i) -> p c t i", i=4))
-        w_code = keep.tile([P, N], U32, name="w_code", tag="words_then_codes", align_bytes=64)
+        w_code = keep.tile([P, N], U32, name="w_code", align_bytes=64)
         w_scale = keep.tile([P, N], U8, name="w_scale", align_bytes=64)
         nc.vector.quantize_mx(out=w_code[:].bitcast(FP8X4), scales=w_scale[:], in_=w_bf[:].rearrange("p n t -> p (n t)"))
 
@@ -107,7 +107,7 @@ def tile_picked_ema_tanh_p_kernel(tc, x_words, x_scales, mem, w1, old, new, offs
                 nc.tensor.transpose(back[:, i, :], scaled[:, i, :], ident[:])
             nc.scalar.copy(target, back[:].rearrange("p i n -> p (i n)"))
 
-        kept = [keep.tile([P, S], F32, name="kept0", tag="w_bf", align_bytes=64), keep.tile([P, S], F32, name="kept1", tag="w_raw")]
+        kept = [shared.tile([P, S], F32, name="kept%d" % b, offset=12288 + 4096 * b) for b in range(BLOCKS)]
         for b in range(BLOCKS):
             nc.vector.tensor_tensor(kept[b][:], mem_sb[b][:].indirect(slot_sb[:]), old_all[:], ALU.mult)
         for b in range(BLOCKS):

@@ -18,9 +18,18 @@ ALU = mybir.AluOpType
 
 P = 128
 PACK = 4
-CHUNKS = S // P
-HALF = S // 2
 BLOCKS = N // P
+CHUNKS = S // P
+PER_BANK = 4
+HALF = PER_BANK * P
+SCALE_ROWS = K // 32
+SCALES_AT = P - SCALE_ROWS
+KEPT_BYTES = 4 * S
+
+NEW_BANK = 0
+SPREAD_BANKS = (1, 2)
+PRODUCT_BANKS = (SPREAD_BANKS, (6, 6))
+BACK_BANKS = ((5, 6), (3, 4))
 
 
 def tile_picked_ema_tanh_p_kernel(tc, x_words, x_scales, mem, w1, old, new, offs, slot, out):
@@ -28,66 +37,70 @@ def tile_picked_ema_tanh_p_kernel(tc, x_words, x_scales, mem, w1, old, new, offs
     with ExitStack() as ctx:
         lists = ctx.enter_context(tc.tile_pool(name="lists", bufs=1))
         keep = ctx.enter_context(tc.tile_pool(name="keep", bufs=1))
+        reused = ctx.enter_context(tc.tile_pool(name="reused", bufs=1))
         psum = ctx.enter_context(tc.psum_pool(name="psum", bufs=1))
-
 
         offs_sb = lists.tile([P, S // 16], U16, name="offs_sb")
         slot_sb = lists.tile([P, S // 16], U16, name="slot_sb")
-        shared = ctx.enter_context(tc.tile_pool(name="shared", bufs=1))
-        scale_tab = shared.tile([P, T], U8, name="scale_tab", offset=3072)
-        ident = keep.tile([P, P], F32, name="ident")
-        old_cols = keep.tile([P, CHUNKS], F32, name="old_cols", tag="w_bf", align_bytes=64)
-        new_rows = keep.tile([P, P], F32, name="new_rows")
+        scale_tab = keep.tile([P, T], U8, name="scale_tab", tag="scales_then_mem")
         word_tab = keep.tile([P, T], U32, name="word_tab")
-        w_raw = shared.tile([P, PACK, N], F32, name="w_raw", offset=14336)
-        mem_sb = [keep.tile([P, U], F32, name="mem0"), shared.tile([P, U], F32, name="mem1", offset=4096)]
+        x_plane = keep.tile([P, S], U8, name="x_plane", align_bytes=64)
+        ident = keep.tile([P, P], F32, name="ident")
+        old_cols = keep.tile([P, CHUNKS], F32, name="old_cols", tag="old_then_w", align_bytes=64)
+        new_rows = keep.tile([P, P], F32, name="new_rows")
+        w_raw = reused.tile([P, PACK, N], F32, name="w_raw", offset=KEPT_BYTES // 2)
+        mem_first = keep.tile([P, U], F32, name="mem_first")
 
         nc.vector.memset(new_rows[:], 0.0)
-        nc.vector.memset(scale_tab[0:112, :].bitcast(I32), 0)
-        x_plane = keep.tile([P, S], U8, name="x_plane", align_bytes=64)
+        nc.vector.memset(scale_tab[0:SCALES_AT, :].bitcast(I32), 0)
         make_identity(nc, ident[:])
         nc.vector.memset(x_plane[:].bitcast(I32), 0)
 
+        nc.sync.dma_start(scale_tab[SCALES_AT:P, :].bitcast(I32), x_scales[0].bitcast(I32))
         nc.sync.dma_start(offs_sb[:], offs)
         nc.scalar.dma_start(old_cols[:], old[0:1, :].rearrange("a (n e) -> (a n) e", e=CHUNKS))
         nc.scalar.dma_start(new_rows[0:CHUNKS, :], new[0:1, :].rearrange("a (c n) -> (a c) n", n=P))
-        nc.sync.dma_start(scale_tab[112:P, :].bitcast(I32), x_scales[0].bitcast(I32))
         nc.sync.dma_start(word_tab[:].bitcast(I32), x_words[0].rearrange("p n t -> p (n t)").bitcast(I32))
-        nc.sync.dma_start(w_raw[:], w1.rearrange("(p j) n -> p j n", j=PACK))
+        nc.sync.dma_start(w_raw[:], w1.rearrange("(p t) n -> p t n", t=PACK))
         nc.sync.dma_start(slot_sb[:], slot)
-        nc.sync.dma_start(mem_sb[0][:], mem[0:P, :])
+        nc.sync.dma_start(mem_first[:], mem[0:P, :])
 
         old_all = keep.tile([P, S], F32, name="old_all")
         for h in range(2):
-            spread = psum.tile([P, 4, P], F32, name="spread", tag="bank%d" % (h + 1))
-            for i in range(4):
-                e = 4 * h + i
+            spread = psum.tile([P, PER_BANK, P], F32, name="spread", tag="bank%d" % SPREAD_BANKS[h])
+            for i in range(PER_BANK):
+                e = PER_BANK * h + i
                 nc.tensor.transpose(spread[:, i, :], old_cols[:, e : e + 1].to_broadcast([P, P]), ident[:])
-            nc.scalar.copy(old_all[:].rearrange("p (n e) -> p n e", e=CHUNKS)[:, :, 4 * h : 4 * h + 4], spread[:].rearrange("p i n -> p n i"))
+            old_by_e = old_all[:].rearrange("p (n e) -> p n e", e=CHUNKS)
+            nc.scalar.copy(old_by_e[:, :, PER_BANK * h : PER_BANK * (h + 1)], spread[:].rearrange("p i n -> p n i"))
 
-        cols_ps = psum.tile([P, 4, P], F32, name="cols_ps", tag="bank0")
-        nc.tensor.transpose(cols_ps[:, 0, :], new_rows[:], ident[:])
+        new_turned = psum.tile([P, P], F32, name="new_turned", tag="bank%d" % NEW_BANK)
+        nc.tensor.transpose(new_turned[:], new_rows[:], ident[:])
         new_cols = keep.tile([P, CHUNKS], F32, name="new_cols")
-        nc.scalar.copy(new_cols[:], cols_ps[:, 0, 0:CHUNKS])
+        nc.scalar.copy(new_cols[:], new_turned[:, 0:CHUNKS])
 
         x_scale = keep.tile([P, S], U8, name="x_scale")
         nc.vector.tensor_copy(x_scale[:], scale_tab[:].indirect(offs_sb[:]))
-        for q in range(4):
-            nc.sync.dma_start(x_plane[32 * q : 32 * q + 4, :].bitcast(I32), x_scale[112 + 4 * q : 116 + 4 * q, :].bitcast(I32))
-        nc.sync.dma_start(mem_sb[1][:], mem[P : 2 * P, :])
+        for q in range(SCALE_ROWS // 4):
+            rows = x_scale[SCALES_AT + 4 * q : SCALES_AT + 4 * q + 4, :]
+            nc.sync.dma_start(x_plane[32 * q : 32 * q + 4, :].bitcast(I32), rows.bitcast(I32))
+        mem_last = keep.tile([P, U], F32, name="mem_last", tag="scales_then_mem")
+        nc.sync.dma_start(mem_last[:], mem[P : 2 * P, :])
+        mem_sb = (mem_first, mem_last)
+
         x_word = keep.tile([P, S], U32, name="x_word", align_bytes=64)
         nc.vector.tensor_copy(x_word[:], word_tab[:].indirect(offs_sb[:]))
 
-        w_bf = keep.tile([P, N, PACK], BF16, name="w_bf", align_bytes=64)
+        w_bf = keep.tile([P, N, PACK], BF16, name="w_bf", tag="old_then_w", align_bytes=64)
         nc.scalar.copy(w_bf[:].rearrange("p (c i) t -> p c t i", i=4), w_raw[:].rearrange("p t (c i) -> p c t i", i=4))
         w_code = keep.tile([P, N], U32, name="w_code", align_bytes=64)
         w_scale = keep.tile([P, N], U8, name="w_scale", align_bytes=64)
         nc.vector.quantize_mx(out=w_code[:].bitcast(FP8X4), scales=w_scale[:], in_=w_bf[:].rearrange("p n t -> p (n t)"))
 
         def fresh_half(b, h, target):
-            z = psum.tile([P, 4, P], F32, name="z", tag="bank%d" % (1 + h))
-            for i in range(4):
-                lo = (4 * h + i) * P
+            z = psum.tile([P, PER_BANK, P], F32, name="z", tag="bank%d" % PRODUCT_BANKS[b][h])
+            for i in range(PER_BANK):
+                lo = (PER_BANK * h + i) * P
                 nc.tensor.matmul_mx(
                     out=z[:, i, :],
                     lhsT=x_word[:, lo : lo + P].bitcast(FP8X4),
@@ -97,19 +110,20 @@ def tile_picked_ema_tanh_p_kernel(tc, x_words, x_scales, mem, w1, old, new, offs
                     start=True,
                     stop=True,
                 )
-            y = keep.tile([P, 4, P], F32, name="y%d%d" % (b, h))
+            y = keep.tile([P, PER_BANK, P], F32, name="y%d%d" % (b, h))
             nc.scalar.activation(y[:], z[:], ACT.Tanh)
-            scaled = keep.tile([P, 4, P], F32, name="scaled%d%d" % (b, h))
-            back = psum.tile([P, 4, P], F32, name="back", tag="bank%d" % (5 + h))
-            for i in range(4):
-                c = 4 * h + i
+            scaled = keep.tile([P, PER_BANK, P], F32, name="scaled%d%d" % (b, h))
+            back = psum.tile([P, PER_BANK, P], F32, name="back", tag="bank%d" % BACK_BANKS[b][h])
+            for i in range(PER_BANK):
+                c = PER_BANK * h + i
                 nc.scalar.activation(scaled[:, i, :], y[:, i, :], ACT.Copy, scale=new_cols[:, c : c + 1])
                 nc.tensor.transpose(back[:, i, :], scaled[:, i, :], ident[:])
             nc.scalar.copy(target, back[:].rearrange("p i n -> p (i n)"))
 
-        kept = [shared.tile([P, S], F32, name="kept%d" % b, offset=12288 + 4096 * b) for b in range(BLOCKS)]
+        kept = [reused.tile([P, S], F32, name="kept%d" % b, offset=KEPT_BYTES * b) for b in range(BLOCKS)]
         for b in range(BLOCKS):
             nc.vector.tensor_tensor(kept[b][:], mem_sb[b][:].indirect(slot_sb[:]), old_all[:], ALU.mult)
+
         for b in range(BLOCKS):
             fresh = keep.tile([P, S], F32, name="fresh%d" % b)
             for h in range(2):

@@ -46,17 +46,19 @@ def tile_picked_ema_tanh_p_kernel(tc, x_words, x_scales, mem, w1, old, new, offs
         word_tab = keep.tile([P, T], U32, name="word_tab")
         x_plane = keep.tile([P, S], U8, name="x_plane", align_bytes=64)
         ident = keep.tile([P, P], F32, name="ident")
-        old_cols = keep.tile([P, CHUNKS], F32, name="old_cols", tag="old_then_w", align_bytes=64)
+        old_cols = keep.tile([P, CHUNKS], F32, name="old_cols")
+        ident_first = keep.tile([P, P], F32, name="ident_first", tag="ident_then_w", align_bytes=64)
         new_rows = keep.tile([P, P], F32, name="new_rows")
         w_raw = reused.tile([P, PACK, N], F32, name="w_raw", offset=KEPT_BYTES // 2)
         mem_first = keep.tile([P, U], F32, name="mem_first")
 
         nc.vector.memset(new_rows[:], 0.0)
         nc.vector.memset(scale_tab[0:SCALES_AT, :].bitcast(I32), 0)
+        make_identity(nc, ident_first[:])
         make_identity(nc, ident[:])
         nc.vector.memset(x_plane[:].bitcast(I32), 0)
 
-        nc.sync.dma_start(scale_tab[SCALES_AT:P, :].bitcast(I32), x_scales[0].bitcast(I32))
+        nc.scalar.dma_start(scale_tab[SCALES_AT:P, :].bitcast(I32), x_scales[0].bitcast(I32))
         nc.sync.dma_start(offs_sb[:], offs)
         nc.scalar.dma_start(old_cols[:], old[0:1, :].rearrange("a (n e) -> (a n) e", e=CHUNKS))
         nc.scalar.dma_start(new_rows[0:CHUNKS, :], new[0:1, :].rearrange("a (c n) -> (a c) n", n=P))
@@ -66,13 +68,18 @@ def tile_picked_ema_tanh_p_kernel(tc, x_words, x_scales, mem, w1, old, new, offs
         nc.sync.dma_start(mem_first[:], mem[0:P, :])
 
         old_all = keep.tile([P, S], F32, name="old_all")
-        for h in range(2):
+        def spread_old(h, identity):
             spread = psum.tile([P, PER_BANK, P], F32, name="spread", tag="bank%d" % SPREAD_BANKS[h])
             for i in range(PER_BANK):
                 e = PER_BANK * h + i
-                nc.tensor.transpose(spread[:, i, :], old_cols[:, e : e + 1].to_broadcast([P, P]), ident[:])
+                nc.tensor.transpose(spread[:, i, :], old_cols[:, e : e + 1].to_broadcast([P, P]), identity[:])
             old_by_e = old_all[:].rearrange("p (n e) -> p n e", e=CHUNKS)
             nc.scalar.copy(old_by_e[:, :, PER_BANK * h : PER_BANK * (h + 1)], spread[:].rearrange("p i n -> p n i"))
+
+        spread_old(0, ident_first)
+        w_bf = keep.tile([P, N, PACK], BF16, name="w_bf", tag="ident_then_w", align_bytes=64)
+        nc.scalar.copy(w_bf[:].rearrange("p (c i) t -> p c t i", i=4), w_raw[:].rearrange("p t (c i) -> p c t i", i=4))
+        spread_old(1, ident)
 
         new_turned = psum.tile([P, P], F32, name="new_turned", tag="bank%d" % NEW_BANK)
         nc.tensor.transpose(new_turned[:], new_rows[:], ident[:])
@@ -91,8 +98,6 @@ def tile_picked_ema_tanh_p_kernel(tc, x_words, x_scales, mem, w1, old, new, offs
         x_word = keep.tile([P, S], U32, name="x_word", align_bytes=64)
         nc.vector.tensor_copy(x_word[:], word_tab[:].indirect(offs_sb[:]))
 
-        w_bf = keep.tile([P, N, PACK], BF16, name="w_bf", tag="old_then_w", align_bytes=64)
-        nc.scalar.copy(w_bf[:].rearrange("p (c i) t -> p c t i", i=4), w_raw[:].rearrange("p t (c i) -> p c t i", i=4))
         w_code = keep.tile([P, N], U32, name="w_code", align_bytes=64)
         w_scale = keep.tile([P, N], U8, name="w_scale", align_bytes=64)
         nc.vector.quantize_mx(out=w_code[:].bitcast(FP8X4), scales=w_scale[:], in_=w_bf[:].rearrange("p n t -> p (n t)"))

@@ -46,51 +46,46 @@ def tile_picked_ema_tanh_p_kernel(tc, x_words, x_scales, mem, w1, old, new, offs
         word_tab = keep.tile([P, T], U32, name="word_tab")
         x_plane = keep.tile([P, S], U8, name="x_plane", align_bytes=64)
         ident = keep.tile([P, P], F32, name="ident")
-        old_cols = keep.tile([P, CHUNKS], F32, name="old_cols")
-        ident_first = keep.tile([P, P], F32, name="ident_first", tag="ident_then_w", align_bytes=64)
-        new_rows = keep.tile([P, P], F32, name="new_rows")
+        rows = keep.tile([P, P], F32, name="rows", tag="rows_then_w", align_bytes=64)
         w_raw = reused.tile([P, PACK, N], F32, name="w_raw", offset=KEPT_BYTES // 2)
         mem_first = keep.tile([P, U], F32, name="mem_first")
 
-        nc.vector.memset(new_rows[:], 0.0)
+        nc.gpsimd.memset(rows[:], 0.0)
         nc.vector.memset(scale_tab[0:SCALES_AT, :].bitcast(I32), 0)
-        make_identity(nc, ident_first[:])
         make_identity(nc, ident[:])
         nc.vector.memset(x_plane[:].bitcast(I32), 0)
 
         nc.scalar.dma_start(scale_tab[SCALES_AT:P, :].bitcast(I32), x_scales[0].bitcast(I32))
         nc.sync.dma_start(offs_sb[:], offs)
-        nc.scalar.dma_start(old_cols[:], old[0:1, :].rearrange("a (n e) -> (a n) e", e=CHUNKS))
-        nc.scalar.dma_start(new_rows[0:CHUNKS, :], new[0:1, :].rearrange("a (c n) -> (a c) n", n=P))
+        nc.scalar.dma_start(rows[0:CHUNKS, :], old[0:1, :].rearrange("a (c n) -> (a c) n", n=P))
+        nc.scalar.dma_start(rows[CHUNKS : 2 * CHUNKS, :], new[0:1, :].rearrange("a (c n) -> (a c) n", n=P))
         nc.sync.dma_start(word_tab[:].bitcast(I32), x_words[0].rearrange("p n t -> p (n t)").bitcast(I32))
-        nc.sync.dma_start(w_raw[:], w1.rearrange("(p t) n -> p t n", t=PACK))
         nc.sync.dma_start(slot_sb[:], slot)
+        nc.sync.dma_start(w_raw[:], w1.rearrange("(p t) n -> p t n", t=PACK))
         nc.sync.dma_start(mem_first[:], mem[0:P, :])
 
+        turned = psum.tile([P, P], F32, name="turned", tag="bank%d" % NEW_BANK)
+        nc.tensor.transpose(turned[:], rows[:], ident[:])
+        cols = keep.tile([P, 2 * CHUNKS], F32, name="cols")
+        nc.scalar.copy(cols[:], turned[:, 0 : 2 * CHUNKS])
+        new_cols = cols[:, CHUNKS : 2 * CHUNKS]
+
+        w_bf = keep.tile([P, N, PACK], BF16, name="w_bf", tag="rows_then_w", align_bytes=64)
+        nc.scalar.copy(w_bf[:].rearrange("p (c i) t -> p c t i", i=4), w_raw[:].rearrange("p t (c i) -> p c t i", i=4))
+
         old_all = keep.tile([P, S], F32, name="old_all")
-        def spread_old(h, identity):
+        for h in range(2):
             spread = psum.tile([P, PER_BANK, P], F32, name="spread", tag="bank%d" % SPREAD_BANKS[h])
             for i in range(PER_BANK):
-                e = PER_BANK * h + i
-                nc.tensor.transpose(spread[:, i, :], old_cols[:, e : e + 1].to_broadcast([P, P]), identity[:])
-            old_by_e = old_all[:].rearrange("p (n e) -> p n e", e=CHUNKS)
-            nc.scalar.copy(old_by_e[:, :, PER_BANK * h : PER_BANK * (h + 1)], spread[:].rearrange("p i n -> p n i"))
-
-        spread_old(0, ident_first)
-        w_bf = keep.tile([P, N, PACK], BF16, name="w_bf", tag="ident_then_w", align_bytes=64)
-        nc.scalar.copy(w_bf[:].rearrange("p (c i) t -> p c t i", i=4), w_raw[:].rearrange("p t (c i) -> p c t i", i=4))
-        spread_old(1, ident)
-
-        new_turned = psum.tile([P, P], F32, name="new_turned", tag="bank%d" % NEW_BANK)
-        nc.tensor.transpose(new_turned[:], new_rows[:], ident[:])
-        new_cols = keep.tile([P, CHUNKS], F32, name="new_cols")
-        nc.scalar.copy(new_cols[:], new_turned[:, 0:CHUNKS])
+                c = PER_BANK * h + i
+                nc.tensor.transpose(spread[:, i, :], cols[:, c : c + 1].to_broadcast([P, P]), ident[:])
+            nc.scalar.copy(old_all[:, h * HALF : (h + 1) * HALF], spread[:].rearrange("p i n -> p (i n)"))
 
         x_scale = keep.tile([P, S], U8, name="x_scale")
         nc.vector.tensor_copy(x_scale[:], scale_tab[:].indirect(offs_sb[:]))
         for q in range(SCALE_ROWS // 4):
-            rows = x_scale[SCALES_AT + 4 * q : SCALES_AT + 4 * q + 4, :]
-            nc.sync.dma_start(x_plane[32 * q : 32 * q + 4, :].bitcast(I32), rows.bitcast(I32))
+            picked = x_scale[SCALES_AT + 4 * q : SCALES_AT + 4 * q + 4, :]
+            nc.sync.dma_start(x_plane[32 * q : 32 * q + 4, :].bitcast(I32), picked.bitcast(I32))
         mem_last = keep.tile([P, U], F32, name="mem_last", tag="scales_then_mem")
         nc.sync.dma_start(mem_last[:], mem[P : 2 * P, :])
         mem_sb = (mem_first, mem_last)
@@ -126,8 +121,11 @@ def tile_picked_ema_tanh_p_kernel(tc, x_words, x_scales, mem, w1, old, new, offs
             nc.scalar.copy(target, back[:].rearrange("p i n -> p (i n)"))
 
         kept = [reused.tile([P, S], F32, name="kept%d" % b, offset=KEPT_BYTES * b) for b in range(BLOCKS)]
-        for b in range(BLOCKS):
-            nc.vector.tensor_tensor(kept[b][:], mem_sb[b][:].indirect(slot_sb[:]), old_all[:], ALU.mult)
+        for h in range(2):
+            half = slice(h * HALF, (h + 1) * HALF)
+            offsets = slot_sb[:, h * HALF // 16 : (h + 1) * HALF // 16]
+            nc.vector.tensor_tensor(kept[0][:, half], mem_first[:].indirect(offsets), old_all[:, half], ALU.mult)
+        nc.vector.tensor_tensor(kept[1][:], mem_last[:].indirect(slot_sb[:]), old_all[:], ALU.mult)
 
         for b in range(BLOCKS):
             fresh = keep.tile([P, S], F32, name="fresh%d" % b)

@@ -57,9 +57,9 @@ def tile_picked_ema_tanh_p_kernel(tc, x_words, x_scales, mem, w1, old, new, offs
 
         nc.scalar.dma_start(scale_tab[SCALES_AT:P, :].bitcast(I32), x_scales[0].bitcast(I32))
         nc.sync.dma_start(offs_sb[:], offs)
-        nc.scalar.dma_start(rows[0:CHUNKS, :], old[0:1, :].rearrange("a (c n) -> (a c) n", n=P))
-        nc.scalar.dma_start(rows[CHUNKS : 2 * CHUNKS, :], new[0:1, :].rearrange("a (c n) -> (a c) n", n=P))
         nc.sync.dma_start(word_tab[:].bitcast(I32), x_words[0].rearrange("p n t -> p (n t)").bitcast(I32))
+        nc.sync.dma_start(rows[0:CHUNKS, :], old[0:1, :].rearrange("a (c n) -> (a c) n", n=P))
+        nc.sync.dma_start(rows[CHUNKS : 2 * CHUNKS, :], new[0:1, :].rearrange("a (c n) -> (a c) n", n=P))
         nc.sync.dma_start(slot_sb[:], slot)
         nc.sync.dma_start(w_raw[:], w1.rearrange("(p t) n -> p t n", t=PACK))
         nc.sync.dma_start(mem_first[:], mem[0:P, :])
@@ -83,9 +83,8 @@ def tile_picked_ema_tanh_p_kernel(tc, x_words, x_scales, mem, w1, old, new, offs
 
         x_scale = keep.tile([P, S], U8, name="x_scale")
         nc.vector.tensor_copy(x_scale[:], scale_tab[:].indirect(offs_sb[:]))
-        for q in range(SCALE_ROWS // 4):
-            picked = x_scale[SCALES_AT + 4 * q : SCALES_AT + 4 * q + 4, :]
-            nc.sync.dma_start(x_plane[32 * q : 32 * q + 4, :].bitcast(I32), picked.bitcast(I32))
+        for r in range(4):
+            nc.sync.dma_start(x_plane[r:P:32, :].bitcast(I32), x_scale[SCALES_AT + r : P : 4, :].bitcast(I32))
         mem_last = keep.tile([P, U], F32, name="mem_last", tag="scales_then_mem")
         nc.sync.dma_start(mem_last[:], mem[P : 2 * P, :])
         mem_sb = (mem_first, mem_last)

@@ -28,8 +28,7 @@ KEPT_BYTES = 4 * S
 
 NEW_BANK = 0
 SPREAD_BANKS = (1, 2)
-PRODUCT_BANKS = (SPREAD_BANKS, (6, 6))
-BACK_BANKS = ((5, 6), (3, 4))
+PIECES = ((0, 0, 4, 2, 3), (1, 0, 4, 2, 4), (0, 4, 4, 2, 5), (1, 4, 4, 2, 6))
 
 
 def tile_picked_ema_tanh_p_kernel(tc, x_words, x_scales, mem, w1, old, new, offs, slot, out):
@@ -96,8 +95,8 @@ def tile_picked_ema_tanh_p_kernel(tc, x_words, x_scales, mem, w1, old, new, offs
         w_scale = keep.tile([P, N], U8, name="w_scale", align_bytes=64)
         nc.vector.quantize_mx(out=w_code[:].bitcast(FP8X4), scales=w_scale[:], in_=w_bf[:].rearrange("p n t -> p (n t)"))
 
-        def fresh_half(b, h, target):
-            z = psum.tile([P, PER_BANK, P], F32, name="z", tag="bank%d" % PRODUCT_BANKS[b][h])
+        def fresh_half(b, h, z_bank, back_bank, target):
+            z = psum.tile([P, PER_BANK, P], F32, name="z", tag="bank%d" % z_bank)
             for i in range(PER_BANK):
                 lo = (PER_BANK * h + i) * P
                 nc.tensor.matmul_mx(
@@ -112,7 +111,7 @@ def tile_picked_ema_tanh_p_kernel(tc, x_words, x_scales, mem, w1, old, new, offs
             y = keep.tile([P, PER_BANK, P], F32, name="y%d%d" % (b, h))
             nc.scalar.activation(y[:], z[:], ACT.Tanh)
             scaled = keep.tile([P, PER_BANK, P], F32, name="scaled%d%d" % (b, h))
-            back = psum.tile([P, PER_BANK, P], F32, name="back", tag="bank%d" % BACK_BANKS[b][h])
+            back = psum.tile([P, PER_BANK, P], F32, name="back", tag="bank%d" % back_bank)
             for i in range(PER_BANK):
                 c = PER_BANK * h + i
                 nc.scalar.activation(scaled[:, i, :], y[:, i, :], ACT.Copy, scale=new_cols[:, c : c + 1])
@@ -126,9 +125,11 @@ def tile_picked_ema_tanh_p_kernel(tc, x_words, x_scales, mem, w1, old, new, offs
             nc.vector.tensor_tensor(kept[0][:, half], mem_first[:].indirect(offsets), old_all[:, half], ALU.mult)
         nc.vector.tensor_tensor(kept[1][:], mem_last[:].indirect(slot_sb[:]), old_all[:], ALU.mult)
 
-        for b in range(BLOCKS):
-            fresh = keep.tile([P, S], F32, name="fresh%d" % b)
-            for h in range(2):
-                fresh_half(b, h, fresh[:, h * HALF : (h + 1) * HALF])
-            nc.vector.tensor_tensor(mem_sb[b][:].indirect(slot_sb[:]), kept[b][:], fresh[:], ALU.add)
-            nc.sync.dma_start(out[b * P : (b + 1) * P, :], mem_sb[b][:])
+        for b, first, count, z_bank, back_bank in PIECES:
+            h = first // PER_BANK
+            fresh = keep.tile([P, HALF], F32, name="fresh%d%d" % (b, h))
+            fresh_half(b, h, z_bank, back_bank, fresh[:])
+            offsets = slot_sb[:, h * HALF // 16 : (h + 1) * HALF // 16]
+            nc.vector.tensor_tensor(mem_sb[b][:].indirect(offsets), kept[b][:, h * HALF : (h + 1) * HALF], fresh[:], ALU.add)
+            if h == 1:
+                nc.sync.dma_start(out[b * P : (b + 1) * P, :], mem_sb[b][:])

@@ -24,11 +24,8 @@ PER_BANK = 4
 HALF = PER_BANK * P
 SCALE_ROWS = K // 32
 SCALES_AT = P - SCALE_ROWS
-KEPT_BYTES = 4 * S
-
-NEW_BANK = 0
-SPREAD_BANKS = (1, 2)
-PIECES = ((0, 0, 4, 2, 3), (1, 0, 4, 2, 4), (0, 4, 4, 2, 5), (1, 4, 4, 2, 6))
+STRIPE = 16
+PIECES = ((0, 384), (384, 768), (768, 1024))
 
 
 def tile_picked_ema_tanh_p_kernel(tc, x_words, x_scales, mem, w1, old, new, offs, slot, out):
@@ -36,18 +33,20 @@ def tile_picked_ema_tanh_p_kernel(tc, x_words, x_scales, mem, w1, old, new, offs
     with ExitStack() as ctx:
         lists = ctx.enter_context(tc.tile_pool(name="lists", bufs=1))
         keep = ctx.enter_context(tc.tile_pool(name="keep", bufs=1))
-        reused = ctx.enter_context(tc.tile_pool(name="reused", bufs=1))
         psum = ctx.enter_context(tc.psum_pool(name="psum", bufs=1))
 
-        offs_sb = lists.tile([P, S // 16], U16, name="offs_sb")
-        slot_sb = lists.tile([P, S // 16], U16, name="slot_sb")
+        offs_sb = lists.tile([P, S // STRIPE], U16, name="offs_sb")
+        slot_sb = lists.tile([P, S // STRIPE], U16, name="slot_sb")
         scale_tab = keep.tile([P, T], U8, name="scale_tab", tag="scales_then_mem")
         word_tab = keep.tile([P, T], U32, name="word_tab")
         x_plane = keep.tile([P, S], U8, name="x_plane", align_bytes=64)
         ident = keep.tile([P, P], F32, name="ident")
         rows = keep.tile([P, P], F32, name="rows", tag="rows_then_w", align_bytes=64)
-        w_raw = reused.tile([P, PACK, N], F32, name="w_raw", offset=KEPT_BYTES // 2)
+        w_raw = keep.tile([P, PACK, N], F32, name="w_raw")
         mem_first = keep.tile([P, U], F32, name="mem_first")
+
+        def slots(lo, hi):
+            return slot_sb[:, lo // STRIPE : hi // STRIPE]
 
         nc.gpsimd.memset(rows[:], 0.0)
         nc.vector.memset(scale_tab[0:SCALES_AT, :].bitcast(I32), 0)
@@ -63,22 +62,24 @@ def tile_picked_ema_tanh_p_kernel(tc, x_words, x_scales, mem, w1, old, new, offs
         nc.sync.dma_start(w_raw[:], w1.rearrange("(p t) n -> p t n", t=PACK))
         nc.sync.dma_start(mem_first[:], mem[0:P, :])
 
-        turned = psum.tile([P, P], F32, name="turned", tag="bank%d" % NEW_BANK)
+        turned = psum.tile([P, P], F32, name="turned", tag="bank4")
         nc.tensor.transpose(turned[:], rows[:], ident[:])
         cols = keep.tile([P, 2 * CHUNKS], F32, name="cols")
         nc.scalar.copy(cols[:], turned[:, 0 : 2 * CHUNKS])
-        new_cols = cols[:, CHUNKS : 2 * CHUNKS]
 
         w_bf = keep.tile([P, N, PACK], BF16, name="w_bf", tag="rows_then_w", align_bytes=64)
         nc.scalar.copy(w_bf[:].rearrange("p (c i) t -> p c t i", i=4), w_raw[:].rearrange("p t (c i) -> p c t i", i=4))
 
+        def spread(first_col, bank):
+            tile = psum.tile([P, PER_BANK, P], F32, name="spread", tag="bank%d" % bank)
+            for i in range(PER_BANK):
+                nc.tensor.transpose(tile[:, i, :], cols[:, first_col + i : first_col + i + 1].to_broadcast([P, P]), ident[:])
+            return tile[:].rearrange("p i n -> p (i n)")
+
         old_all = keep.tile([P, S], F32, name="old_all")
         for h in range(2):
-            spread = psum.tile([P, PER_BANK, P], F32, name="spread", tag="bank%d" % SPREAD_BANKS[h])
-            for i in range(PER_BANK):
-                c = PER_BANK * h + i
-                nc.tensor.transpose(spread[:, i, :], cols[:, c : c + 1].to_broadcast([P, P]), ident[:])
-            nc.scalar.copy(old_all[:, h * HALF : (h + 1) * HALF], spread[:].rearrange("p i n -> p (i n)"))
+            nc.scalar.copy(old_all[:, h * HALF : (h + 1) * HALF], spread(PER_BANK * h, h))
+        new_half = [spread(CHUNKS + PER_BANK * h, 2 + h) for h in range(2)]
 
         x_scale = keep.tile([P, S], U8, name="x_scale")
         nc.vector.tensor_copy(x_scale[:], scale_tab[:].indirect(offs_sb[:]))
@@ -86,7 +87,6 @@ def tile_picked_ema_tanh_p_kernel(tc, x_words, x_scales, mem, w1, old, new, offs
             nc.sync.dma_start(x_plane[r:P:32, :].bitcast(I32), x_scale[SCALES_AT + r : P : 4, :].bitcast(I32))
         mem_last = keep.tile([P, U], F32, name="mem_last", tag="scales_then_mem")
         nc.sync.dma_start(mem_last[:], mem[P : 2 * P, :])
-        mem_sb = (mem_first, mem_last)
 
         x_word = keep.tile([P, S], U32, name="x_word", align_bytes=64)
         nc.vector.tensor_copy(x_word[:], word_tab[:].indirect(offs_sb[:]))
@@ -95,41 +95,40 @@ def tile_picked_ema_tanh_p_kernel(tc, x_words, x_scales, mem, w1, old, new, offs
         w_scale = keep.tile([P, N], U8, name="w_scale", align_bytes=64)
         nc.vector.quantize_mx(out=w_code[:].bitcast(FP8X4), scales=w_scale[:], in_=w_bf[:].rearrange("p n t -> p (n t)"))
 
-        def fresh_half(b, h, z_bank, back_bank, target):
-            z = psum.tile([P, PER_BANK, P], F32, name="z", tag="bank%d" % z_bank)
-            for i in range(PER_BANK):
-                lo = (PER_BANK * h + i) * P
+        kept_first = keep.tile([P, S], F32, name="kept_first")
+        nc.vector.tensor_tensor(kept_first[:], mem_first[:].indirect(slot_sb[:]), old_all[:], ALU.mult)
+
+        y = [keep.tile([P, S], F32, name="y%d" % b) for b in range(BLOCKS)]
+        for b in range(BLOCKS):
+            for h in range(2):
+                half = slice(h * HALF, (h + 1) * HALF)
+                z = psum.tile([P, HALF], F32, name="z", tag="bank%d" % (4 + 2 * b + h))
                 nc.tensor.matmul_mx(
-                    out=z[:, i, :],
-                    lhsT=x_word[:, lo : lo + P].bitcast(FP8X4),
-                    lhsT_scale=x_plane[:, lo : lo + P],
-                    rhs=w_code[:, b * P : (b + 1) * P].bitcast(FP8X4),
-                    rhs_scale=w_scale[:, b * P : (b + 1) * P],
+                    out=z[:],
+                    lhsT=w_code[:, b * P : (b + 1) * P].bitcast(FP8X4),
+                    lhsT_scale=w_scale[:, b * P : (b + 1) * P],
+                    rhs=x_word[:, half].bitcast(FP8X4),
+                    rhs_scale=x_plane[:, half],
                     start=True,
                     stop=True,
                 )
-            y = keep.tile([P, PER_BANK, P], F32, name="y%d%d" % (b, h))
-            nc.scalar.activation(y[:], z[:], ACT.Tanh)
-            scaled = keep.tile([P, PER_BANK, P], F32, name="scaled%d%d" % (b, h))
-            back = psum.tile([P, PER_BANK, P], F32, name="back", tag="bank%d" % back_bank)
-            for i in range(PER_BANK):
-                c = PER_BANK * h + i
-                nc.scalar.activation(scaled[:, i, :], y[:, i, :], ACT.Copy, scale=new_cols[:, c : c + 1])
-                nc.tensor.transpose(back[:, i, :], scaled[:, i, :], ident[:])
-            nc.scalar.copy(target, back[:].rearrange("p i n -> p (i n)"))
+                nc.scalar.activation(y[b][:, half], z[:], ACT.Tanh)
 
-        kept = [reused.tile([P, S], F32, name="kept%d" % b, offset=KEPT_BYTES * b) for b in range(BLOCKS)]
-        for h in range(2):
-            half = slice(h * HALF, (h + 1) * HALF)
-            offsets = slot_sb[:, h * HALF // 16 : (h + 1) * HALF // 16]
-            nc.vector.tensor_tensor(kept[0][:, half], mem_first[:].indirect(offsets), old_all[:, half], ALU.mult)
-        nc.vector.tensor_tensor(kept[1][:], mem_last[:].indirect(slot_sb[:]), old_all[:], ALU.mult)
+        picked_last = keep.tile([P, S], F32, name="picked_last")
+        nc.scalar.activation(picked_last[:], mem_last[:].indirect(slot_sb[:]), ACT.Copy)
 
-        for b, first, count, z_bank, back_bank in PIECES:
-            h = first // PER_BANK
-            fresh = keep.tile([P, HALF], F32, name="fresh%d%d" % (b, h))
-            fresh_half(b, h, z_bank, back_bank, fresh[:])
-            offsets = slot_sb[:, h * HALF // 16 : (h + 1) * HALF // 16]
-            nc.vector.tensor_tensor(mem_sb[b][:].indirect(offsets), kept[b][:, h * HALF : (h + 1) * HALF], fresh[:], ALU.add)
-            if h == 1:
-                nc.sync.dma_start(out[b * P : (b + 1) * P, :], mem_sb[b][:])
+        fresh = [keep.tile([P, S], F32, name="fresh%d" % b) for b in range(BLOCKS)]
+        for b in range(BLOCKS):
+            for h in range(2):
+                half = slice(h * HALF, (h + 1) * HALF)
+                nc.vector.tensor_tensor(fresh[b][:, half], y[b][:, half], new_half[h], ALU.mult)
+        sum_first = keep.tile([P, S], F32, name="sum_first")
+        nc.vector.tensor_tensor(sum_first[:], kept_first[:], fresh[0][:], ALU.add)
+        kept_last = keep.tile([P, S], F32, name="kept_last")
+        nc.vector.tensor_tensor(kept_last[:], picked_last[:], old_all[:], ALU.mult)
+
+        for lo, hi in PIECES:
+            nc.scalar.activation(mem_first[:].indirect(slots(lo, hi)), sum_first[:, lo:hi], ACT.Copy)
+        nc.sync.dma_start(out[0:P, :], mem_first[:])
+        nc.vector.tensor_tensor(mem_last[:].indirect(slot_sb[:]), kept_last[:], fresh[1][:], ALU.add)
+        nc.sync.dma_start(out[P : 2 * P, :], mem_last[:])

@@ -25,6 +25,7 @@ HALF = PER_BANK * P
 SCALE_ROWS = K // 32
 SCALES_AT = P - SCALE_ROWS
 STRIPE = 16
+FUSED = (576, 448)
 PIECES = ((0, 384), (384, 768), (768, 1024))
 
 
@@ -76,10 +77,11 @@ def tile_picked_ema_tanh_p_kernel(tc, x_words, x_scales, mem, w1, old, new, offs
                 nc.tensor.transpose(tile[:, i, :], cols[:, first_col + i : first_col + i + 1].to_broadcast([P, P]), ident[:])
             return tile[:].rearrange("p i n -> p (i n)")
 
-        old_all = keep.tile([P, S], F32, name="old_all")
+        old_then_sum = keep.tile([P, 2 * S - FUSED[1] - PIECES[0][1]], F32, name="old_then_sum")
+        old_all = old_then_sum[:, 0:S]
         for h in range(2):
             nc.scalar.copy(old_all[:, h * HALF : (h + 1) * HALF], spread(PER_BANK * h, h))
-        new_half = [spread(CHUNKS + PER_BANK * h, 2 + h) for h in range(2)]
+        new_half = [spread(CHUNKS, 2)]
 
         x_scale = keep.tile([P, S], U8, name="x_scale")
         nc.vector.tensor_copy(x_scale[:], scale_tab[:].indirect(offs_sb[:]))
@@ -96,7 +98,11 @@ def tile_picked_ema_tanh_p_kernel(tc, x_words, x_scales, mem, w1, old, new, offs
         nc.vector.quantize_mx(out=w_code[:].bitcast(FP8X4), scales=w_scale[:], in_=w_bf[:].rearrange("p n t -> p (n t)"))
 
         kept_first = keep.tile([P, S], F32, name="kept_first")
-        nc.vector.tensor_tensor(kept_first[:], mem_first[:].indirect(slot_sb[:]), old_all[:], ALU.mult)
+        cut = FUSED[0]
+        picked_first = keep.tile([P, S - cut], F32, name="picked_first")
+        nc.scalar.activation(picked_first[:], mem_first[:].indirect(slots(cut, S)), ACT.Copy)
+        nc.vector.tensor_tensor(kept_first[:, 0:cut], mem_first[:].indirect(slots(0, cut)), old_all[:, 0:cut], ALU.mult)
+        nc.vector.tensor_tensor(kept_first[:, cut:S], picked_first[:], old_all[:, cut:S], ALU.mult)
 
         y = [keep.tile([P, S], F32, name="y%d" % b) for b in range(BLOCKS)]
         for b in range(BLOCKS):
@@ -114,21 +120,33 @@ def tile_picked_ema_tanh_p_kernel(tc, x_words, x_scales, mem, w1, old, new, offs
                 )
                 nc.scalar.activation(y[b][:, half], z[:], ACT.Tanh)
 
-        picked_last = keep.tile([P, S], F32, name="picked_last")
-        nc.scalar.activation(picked_last[:], mem_last[:].indirect(slot_sb[:]), ACT.Copy)
+        new_half.append(spread(CHUNKS + PER_BANK, 4))
+        cut = S - FUSED[1]
+        picked_last = keep.tile([P, cut], F32, name="picked_last")
+        nc.scalar.activation(picked_last[:], mem_last[:].indirect(slots(0, cut)), ACT.Copy)
 
         fresh = [keep.tile([P, S], F32, name="fresh%d" % b) for b in range(BLOCKS)]
-        for b in range(BLOCKS):
-            for h in range(2):
-                half = slice(h * HALF, (h + 1) * HALF)
-                nc.vector.tensor_tensor(fresh[b][:, half], y[b][:, half], new_half[h], ALU.mult)
-        sum_first = keep.tile([P, S], F32, name="sum_first")
-        nc.vector.tensor_tensor(sum_first[:], kept_first[:], fresh[0][:], ALU.add)
+        halves = [slice(h * HALF, (h + 1) * HALF) for h in range(2)]
+
+        def times_new(b, h):
+            nc.vector.tensor_tensor(fresh[b][:, halves[h]], y[b][:, halves[h]], new_half[h], ALU.mult)
+
         kept_last = keep.tile([P, S], F32, name="kept_last")
-        nc.vector.tensor_tensor(kept_last[:], picked_last[:], old_all[:], ALU.mult)
+        head = PIECES[0][1]
+        sum_head = keep.tile([P, head], F32, name="sum_head")
+        sum_rest = old_then_sum[:, cut : cut + S - head]
+        times_new(0, 0)
+        times_new(0, 1)
+        nc.vector.tensor_tensor(sum_head[:], kept_first[:, 0:head], fresh[0][:, 0:head], ALU.add)
+        times_new(1, 0)
+        nc.vector.tensor_tensor(kept_last[:, cut:S], mem_last[:].indirect(slots(cut, S)), old_all[:, cut:S], ALU.mult)
+        times_new(1, 1)
+        nc.vector.tensor_tensor(sum_rest, kept_first[:, head:S], fresh[0][:, head:S], ALU.add)
+        nc.vector.tensor_tensor(kept_last[:, 0:cut], picked_last[:], old_all[:, 0:cut], ALU.mult)
 
         for lo, hi in PIECES:
-            nc.scalar.activation(mem_first[:].indirect(slots(lo, hi)), sum_first[:, lo:hi], ACT.Copy)
+            source = sum_head[:] if lo == 0 else sum_rest[:, lo - head : hi - head]
+            nc.scalar.activation(mem_first[:].indirect(slots(lo, hi)), source, ACT.Copy)
         nc.sync.dma_start(out[0:P, :], mem_first[:])
         nc.vector.tensor_tensor(mem_last[:].indirect(slot_sb[:]), kept_last[:], fresh[1][:], ALU.add)
         nc.sync.dma_start(out[P : 2 * P, :], mem_last[:])

@@ -25,7 +25,7 @@ HALF = PER_BANK * P
 SCALE_ROWS = K // 32
 SCALES_AT = P - SCALE_ROWS
 STRIPE = 16
-FUSED = (576, 448)
+FUSED = (576, 576)
 PIECES = ((0, 384), (384, 768), (768, 1024))
 
 
@@ -105,8 +105,8 @@ def tile_picked_ema_tanh_p_kernel(tc, x_words, x_scales, mem, w1, old, new, offs
         nc.vector.tensor_tensor(kept_first[:, cut:S], picked_first[:], old_all[:, cut:S], ALU.mult)
 
         y = [keep.tile([P, S], F32, name="y%d" % b) for b in range(BLOCKS)]
-        for b in range(BLOCKS):
-            for h in range(2):
+        for h in range(2):
+            for b in range(BLOCKS):
                 half = slice(h * HALF, (h + 1) * HALF)
                 z = psum.tile([P, HALF], F32, name="z", tag="bank%d" % (4 + 2 * b + h))
                 nc.tensor.matmul_mx(
@@ -136,17 +136,19 @@ def tile_picked_ema_tanh_p_kernel(tc, x_words, x_scales, mem, w1, old, new, offs
         sum_head = keep.tile([P, head], F32, name="sum_head")
         sum_rest = old_then_sum[:, cut : cut + S - head]
         times_new(0, 0)
-        times_new(0, 1)
-        nc.vector.tensor_tensor(sum_head[:], kept_first[:, 0:head], fresh[0][:, 0:head], ALU.add)
         times_new(1, 0)
+        nc.vector.tensor_tensor(sum_head[:], kept_first[:, 0:head], fresh[0][:, 0:head], ALU.add)
+        times_new(0, 1)
         nc.vector.tensor_tensor(kept_last[:, cut:S], mem_last[:].indirect(slots(cut, S)), old_all[:, cut:S], ALU.mult)
         times_new(1, 1)
-        nc.vector.tensor_tensor(sum_rest, kept_first[:, head:S], fresh[0][:, head:S], ALU.add)
+        tail = PIECES[2][0]
+        nc.vector.tensor_tensor(sum_rest[:, 0 : tail - head], kept_first[:, head:tail], fresh[0][:, head:tail], ALU.add)
         nc.vector.tensor_tensor(kept_last[:, 0:cut], picked_last[:], old_all[:, 0:cut], ALU.mult)
+        nc.vector.tensor_tensor(sum_rest[:, tail - head : S - head], kept_first[:, tail:S], fresh[0][:, tail:S], ALU.add)
 
         for lo, hi in PIECES:
             source = sum_head[:] if lo == 0 else sum_rest[:, lo - head : hi - head]
             nc.scalar.activation(mem_first[:].indirect(slots(lo, hi)), source, ACT.Copy)
-        nc.sync.dma_start(out[0:P, :], mem_first[:])
+        nc.scalar.dma_start(out[0:P, :], mem_first[:])
         nc.vector.tensor_tensor(mem_last[:].indirect(slot_sb[:]), kept_last[:], fresh[1][:], ALU.add)
         nc.sync.dma_start(out[P : 2 * P, :], mem_last[:])

@@ -25,8 +25,8 @@ HALF = PER_BANK * P
 SCALE_ROWS = K // 32
 SCALES_AT = P - SCALE_ROWS
 STRIPE = 16
-FUSED = (576, 576)
-PIECES = ((0, 384), (384, 768), (768, 1024))
+FUSED = (704, 640)
+PIECES = ((0, 384), (384, 640), (640, 1024))
 
 
 def tile_picked_ema_tanh_p_kernel(tc, x_words, x_scales, mem, w1, old, new, offs, slot, out):
@@ -77,10 +77,10 @@ def tile_picked_ema_tanh_p_kernel(tc, x_words, x_scales, mem, w1, old, new, offs
                 nc.tensor.transpose(tile[:, i, :], cols[:, first_col + i : first_col + i + 1].to_broadcast([P, P]), ident[:])
             return tile[:].rearrange("p i n -> p (i n)")
 
-        old_then_sum = keep.tile([P, 2 * S - FUSED[1] - PIECES[0][1]], F32, name="old_then_sum")
-        old_all = old_then_sum[:, 0:S]
+        old_all = keep.tile([P, S], F32, name="old_all")
+        old_half = [spread(PER_BANK * h, h) for h in range(2)]
         for h in range(2):
-            nc.scalar.copy(old_all[:, h * HALF : (h + 1) * HALF], spread(PER_BANK * h, h))
+            nc.scalar.copy(old_all[:, h * HALF : (h + 1) * HALF], old_half[h])
         new_half = [spread(CHUNKS, 2)]
 
         x_scale = keep.tile([P, S], U8, name="x_scale")
@@ -102,25 +102,24 @@ def tile_picked_ema_tanh_p_kernel(tc, x_words, x_scales, mem, w1, old, new, offs
         picked_first = keep.tile([P, S - cut], F32, name="picked_first")
         nc.scalar.activation(picked_first[:], mem_first[:].indirect(slots(cut, S)), ACT.Copy)
         nc.vector.tensor_tensor(kept_first[:, 0:cut], mem_first[:].indirect(slots(0, cut)), old_all[:, 0:cut], ALU.mult)
-        nc.vector.tensor_tensor(kept_first[:, cut:S], picked_first[:], old_all[:, cut:S], ALU.mult)
+        nc.gpsimd.tensor_tensor(kept_first[:, cut:S], picked_first[:], old_all[:, cut:S], ALU.mult)
 
         y = [keep.tile([P, S], F32, name="y%d" % b) for b in range(BLOCKS)]
-        for h in range(2):
-            for b in range(BLOCKS):
-                half = slice(h * HALF, (h + 1) * HALF)
-                z = psum.tile([P, HALF], F32, name="z", tag="bank%d" % (4 + 2 * b + h))
-                nc.tensor.matmul_mx(
-                    out=z[:],
-                    lhsT=w_code[:, b * P : (b + 1) * P].bitcast(FP8X4),
-                    lhsT_scale=w_scale[:, b * P : (b + 1) * P],
-                    rhs=x_word[:, half].bitcast(FP8X4),
-                    rhs_scale=x_plane[:, half],
-                    start=True,
-                    stop=True,
-                )
-                nc.scalar.activation(y[b][:, half], z[:], ACT.Tanh)
+        units = ((0, 0, HALF // 2, 3), (0, HALF // 2, HALF, 4), (1, 0, HALF, 6), (0, HALF, S, 5), (1, HALF, S, 7))
+        for b, lo, hi, bank in units:
+            z = psum.tile([P, hi - lo], F32, name="z", tag="bank%d" % bank)
+            nc.tensor.matmul_mx(
+                out=z[:],
+                lhsT=w_code[:, b * P : (b + 1) * P].bitcast(FP8X4),
+                lhsT_scale=w_scale[:, b * P : (b + 1) * P],
+                rhs=x_word[:, lo:hi].bitcast(FP8X4),
+                rhs_scale=x_plane[:, lo:hi],
+                start=True,
+                stop=True,
+            )
+            nc.scalar.activation(y[b][:, lo:hi], z[:], ACT.Tanh)
 
-        new_half.append(spread(CHUNKS + PER_BANK, 4))
+        new_half.append(spread(CHUNKS + PER_BANK, 3))
         cut = S - FUSED[1]
         picked_last = keep.tile([P, cut], F32, name="picked_last")
         nc.scalar.activation(picked_last[:], mem_last[:].indirect(slots(0, cut)), ACT.Copy)
@@ -132,22 +131,21 @@ def tile_picked_ema_tanh_p_kernel(tc, x_words, x_scales, mem, w1, old, new, offs
             nc.vector.tensor_tensor(fresh[b][:, halves[h]], y[b][:, halves[h]], new_half[h], ALU.mult)
 
         kept_last = keep.tile([P, S], F32, name="kept_last")
-        head = PIECES[0][1]
+        head, tail = PIECES[1]
         sum_head = keep.tile([P, head], F32, name="sum_head")
-        sum_rest = old_then_sum[:, cut : cut + S - head]
+        sum_mid = keep.tile([P, tail - head], F32, name="sum_mid")
+        sum_tail = old_all[:, cut : cut + S - tail]
         times_new(0, 0)
         times_new(1, 0)
         nc.vector.tensor_tensor(sum_head[:], kept_first[:, 0:head], fresh[0][:, 0:head], ALU.add)
         times_new(0, 1)
         nc.vector.tensor_tensor(kept_last[:, cut:S], mem_last[:].indirect(slots(cut, S)), old_all[:, cut:S], ALU.mult)
+        nc.gpsimd.tensor_tensor(sum_tail, kept_first[:, tail:S], fresh[0][:, tail:S], ALU.add)
+        nc.vector.tensor_tensor(sum_mid[:], kept_first[:, head:tail], fresh[0][:, head:tail], ALU.add)
         times_new(1, 1)
-        tail = PIECES[2][0]
-        nc.vector.tensor_tensor(sum_rest[:, 0 : tail - head], kept_first[:, head:tail], fresh[0][:, head:tail], ALU.add)
-        nc.vector.tensor_tensor(kept_last[:, 0:cut], picked_last[:], old_all[:, 0:cut], ALU.mult)
-        nc.vector.tensor_tensor(sum_rest[:, tail - head : S - head], kept_first[:, tail:S], fresh[0][:, tail:S], ALU.add)
+        nc.vector.tensor_tensor(kept_last[:, 0:cut], picked_last[:], old_half[0][:, 0:cut], ALU.mult)
 
-        for lo, hi in PIECES:
-            source = sum_head[:] if lo == 0 else sum_rest[:, lo - head : hi - head]
+        for (lo, hi), source in zip(PIECES, (sum_head[:], sum_mid[:], sum_tail)):
             nc.scalar.activation(mem_first[:].indirect(slots(lo, hi)), source, ACT.Copy)
         nc.scalar.dma_start(out[0:P, :], mem_first[:])
         nc.vector.tensor_tensor(mem_last[:].indirect(slot_sb[:]), kept_last[:], fresh[1][:], ALU.add)

@@ -18,15 +18,15 @@ ALU = mybir.AluOpType
 
 P = 128
 PACK = 4
-BLOCKS = N // P
 CHUNKS = S // P
 PER_BANK = 4
 HALF = PER_BANK * P
 SCALE_ROWS = K // 32
 SCALES_AT = P - SCALE_ROWS
 STRIPE = 16
-FUSED = (704, 640)
-PIECES = ((0, 384), (384, 640), (640, 1024))
+CUT_A, CUT_B = 384, 640
+SPARE = 128
+PICK1 = 384
 
 
 def tile_picked_ema_tanh_p_kernel(tc, x_words, x_scales, mem, w1, old, new, offs, slot, out):
@@ -34,17 +34,18 @@ def tile_picked_ema_tanh_p_kernel(tc, x_words, x_scales, mem, w1, old, new, offs
     with ExitStack() as ctx:
         lists = ctx.enter_context(tc.tile_pool(name="lists", bufs=1))
         keep = ctx.enter_context(tc.tile_pool(name="keep", bufs=1))
+        laid = ctx.enter_context(tc.tile_pool(name="laid", bufs=1))
         psum = ctx.enter_context(tc.psum_pool(name="psum", bufs=1))
 
         offs_sb = lists.tile([P, S // STRIPE], U16, name="offs_sb")
         slot_sb = lists.tile([P, S // STRIPE], U16, name="slot_sb")
-        scale_tab = keep.tile([P, T], U8, name="scale_tab", tag="scales_then_mem")
+        scale_tab = laid.tile([P, T], U8, name="scale_tab", offset=T // 2)
         word_tab = keep.tile([P, T], U32, name="word_tab")
         x_plane = keep.tile([P, S], U8, name="x_plane", align_bytes=64)
         ident = keep.tile([P, P], F32, name="ident")
         rows = keep.tile([P, P], F32, name="rows", tag="rows_then_w", align_bytes=64)
-        w_raw = keep.tile([P, PACK, N], F32, name="w_raw")
-        mem_first = keep.tile([P, U], F32, name="mem_first")
+        w_raw = keep.tile([P, PACK, N], F32, name="w_raw", tag="w_then_picked")
+        mem0 = keep.tile([P, U], F32, name="mem0")
 
         def slots(lo, hi):
             return slot_sb[:, lo // STRIPE : hi // STRIPE]
@@ -58,15 +59,15 @@ def tile_picked_ema_tanh_p_kernel(tc, x_words, x_scales, mem, w1, old, new, offs
         nc.sync.dma_start(offs_sb[:], offs)
         nc.sync.dma_start(word_tab[:].bitcast(I32), x_words[0].rearrange("p n t -> p (n t)").bitcast(I32))
         nc.sync.dma_start(rows[0:CHUNKS, :], old[0:1, :].rearrange("a (c n) -> (a c) n", n=P))
-        nc.sync.dma_start(rows[CHUNKS : 2 * CHUNKS, :], new[0:1, :].rearrange("a (c n) -> (a c) n", n=P))
+        nc.sync.dma_start(rows[CHUNKS : CHUNKS + PER_BANK, :], new[0:1, 0:HALF].rearrange("a (c n) -> (a c) n", n=P))
         nc.sync.dma_start(slot_sb[:], slot)
         nc.sync.dma_start(w_raw[:], w1.rearrange("(p t) n -> p t n", t=PACK))
-        nc.sync.dma_start(mem_first[:], mem[0:P, :])
+        nc.sync.dma_start(mem0[:], mem[0:P, :])
 
         turned = psum.tile([P, P], F32, name="turned", tag="bank4")
         nc.tensor.transpose(turned[:], rows[:], ident[:])
-        cols = keep.tile([P, 2 * CHUNKS], F32, name="cols")
-        nc.scalar.copy(cols[:], turned[:, 0 : 2 * CHUNKS])
+        cols = keep.tile([P, CHUNKS + PER_BANK], F32, name="cols")
+        nc.scalar.copy(cols[:], turned[:, 0 : CHUNKS + PER_BANK])
 
         w_bf = keep.tile([P, N, PACK], BF16, name="w_bf", tag="rows_then_w", align_bytes=64)
         nc.scalar.copy(w_bf[:].rearrange("p (c i) t -> p c t i", i=4), w_raw[:].rearrange("p t (c i) -> p c t i", i=4))
@@ -77,18 +78,19 @@ def tile_picked_ema_tanh_p_kernel(tc, x_words, x_scales, mem, w1, old, new, offs
                 nc.tensor.transpose(tile[:, i, :], cols[:, first_col + i : first_col + i + 1].to_broadcast([P, P]), ident[:])
             return tile[:].rearrange("p i n -> p (i n)")
 
-        old_all = keep.tile([P, S], F32, name="old_all")
-        old_half = [spread(PER_BANK * h, h) for h in range(2)]
-        for h in range(2):
-            nc.scalar.copy(old_all[:, h * HALF : (h + 1) * HALF], old_half[h])
-        new_half = [spread(CHUNKS, 2)]
+        old_sb = keep.tile([P, S], F32, name="old_sb")
+        nc.scalar.copy(old_sb[:, 0:HALF], spread(0, 0))
+        old_hi = spread(PER_BANK, 1)
+        new_lo = spread(CHUNKS, 2)
 
         x_scale = keep.tile([P, S], U8, name="x_scale")
         nc.vector.tensor_copy(x_scale[:], scale_tab[:].indirect(offs_sb[:]))
         for r in range(4):
             nc.sync.dma_start(x_plane[r:P:32, :].bitcast(I32), x_scale[SCALES_AT + r : P : 4, :].bitcast(I32))
-        mem_last = keep.tile([P, U], F32, name="mem_last", tag="scales_then_mem")
-        nc.sync.dma_start(mem_last[:], mem[P : 2 * P, :])
+        mem1 = laid.tile([P, U], F32, name="mem1", offset=T)
+        nc.sync.dma_start(mem1[:], mem[P : 2 * P, :])
+        new_hi = laid.tile([P, HALF], F32, name="new_hi", offset=0)
+        nc.sync.dma_start(new_hi[:], new[:, HALF:S])
 
         x_word = keep.tile([P, S], U32, name="x_word", align_bytes=64)
         nc.vector.tensor_copy(x_word[:], word_tab[:].indirect(offs_sb[:]))
@@ -96,17 +98,9 @@ def tile_picked_ema_tanh_p_kernel(tc, x_words, x_scales, mem, w1, old, new, offs
         w_code = keep.tile([P, N], U32, name="w_code", align_bytes=64)
         w_scale = keep.tile([P, N], U8, name="w_scale", align_bytes=64)
         nc.vector.quantize_mx(out=w_code[:].bitcast(FP8X4), scales=w_scale[:], in_=w_bf[:].rearrange("p n t -> p (n t)"))
+        nc.vector.tensor_copy(old_sb[:, HALF:S], old_hi)
 
-        kept_first = keep.tile([P, S], F32, name="kept_first")
-        cut = FUSED[0]
-        picked_first = keep.tile([P, S - cut], F32, name="picked_first")
-        nc.scalar.activation(picked_first[:], mem_first[:].indirect(slots(cut, S)), ACT.Copy)
-        nc.vector.tensor_tensor(kept_first[:, 0:cut], mem_first[:].indirect(slots(0, cut)), old_all[:, 0:cut], ALU.mult)
-        nc.gpsimd.tensor_tensor(kept_first[:, cut:S], picked_first[:], old_all[:, cut:S], ALU.mult)
-
-        y = [keep.tile([P, S], F32, name="y%d" % b) for b in range(BLOCKS)]
-        units = ((0, 0, HALF // 2, 3), (0, HALF // 2, HALF, 4), (1, 0, HALF, 6), (0, HALF, S, 5), (1, HALF, S, 7))
-        for b, lo, hi, bank in units:
+        def tanh_of_product(dst, b, lo, hi, bank):
             z = psum.tile([P, hi - lo], F32, name="z", tag="bank%d" % bank)
             nc.tensor.matmul_mx(
                 out=z[:],
@@ -117,36 +111,60 @@ def tile_picked_ema_tanh_p_kernel(tc, x_words, x_scales, mem, w1, old, new, offs
                 start=True,
                 stop=True,
             )
-            nc.scalar.activation(y[b][:, lo:hi], z[:], ACT.Tanh)
+            nc.scalar.activation(dst, z[:], ACT.Tanh)
 
-        new_half.append(spread(CHUNKS + PER_BANK, 3))
-        cut = S - FUSED[1]
-        picked_last = keep.tile([P, cut], F32, name="picked_last")
-        nc.scalar.activation(picked_last[:], mem_last[:].indirect(slots(0, cut)), ACT.Copy)
+        fused = HALF - PICK1
+        cut1 = S - PICK1
+        work = keep.tile([P, S + HALF], F32, name="work")
+        fresh0 = work[:, 0:S]
+        kept1_lo = work[:, S : S + HALF]
+        y1_lo = work[:, S - HALF // 2 : S + HALF // 2]
+        mid = CUT_B + SPARE
+        fresh1_hi = work[:, mid : mid + HALF]
+        last = keep.tile([P, 2 * (S - CUT_B) - SPARE], F32, name="last")
+        sum_c = last[:, 0 : S - CUT_B]
+        kept0_c = last[:, S - CUT_B - SPARE : 2 * (S - CUT_B) - SPARE]
+        y0 = keep.tile([P, S], F32, name="y0")
+        picked1 = y0[:, 0:PICK1]
+        y1_hi = y0[:, HALF:S]
+        kept0 = keep.tile([P, CUT_B], F32, name="kept0")
+        kept1_hi = work[:, mid - HALF : mid]
+        picked0 = keep.tile([P, S - CUT_B], F32, name="picked0", tag="w_then_picked")
+        fresh1_lo = keep.tile([P, HALF], F32, name="fresh1_lo")
+        sum1_lo = keep.tile([P, HALF], F32, name="sum1_lo")
+        sum_a = keep.tile([P, CUT_A], F32, name="sum_a")
+        sum_b = keep.tile([P, CUT_B - CUT_A], F32, name="sum_b")
 
-        fresh = [keep.tile([P, S], F32, name="fresh%d" % b) for b in range(BLOCKS)]
-        halves = [slice(h * HALF, (h + 1) * HALF) for h in range(2)]
+        nc.scalar.activation(picked0[:], mem0[:].indirect(slots(CUT_B, S)), ACT.Copy)
+        nc.vector.tensor_tensor(kept0[:, 0:CUT_B], mem0[:].indirect(slots(0, CUT_B)), old_sb[:, 0:CUT_B], ALU.mult)
+        nc.gpsimd.tensor_tensor(kept0_c, picked0[:], old_sb[:, CUT_B:S], ALU.mult)
 
-        def times_new(b, h):
-            nc.vector.tensor_tensor(fresh[b][:, halves[h]], y[b][:, halves[h]], new_half[h], ALU.mult)
+        tanh_of_product(y0[:, 0 : HALF // 2], 0, 0, HALF // 2, 3)
+        tanh_of_product(y0[:, HALF // 2 : HALF], 0, HALF // 2, HALF, 4)
+        tanh_of_product(y1_lo, 1, 0, HALF, 5)
+        tanh_of_product(y0[:, HALF:S], 0, HALF, S, 6)
 
-        kept_last = keep.tile([P, S], F32, name="kept_last")
-        head, tail = PIECES[1]
-        sum_head = keep.tile([P, head], F32, name="sum_head")
-        sum_mid = keep.tile([P, tail - head], F32, name="sum_mid")
-        sum_tail = old_all[:, cut : cut + S - tail]
-        times_new(0, 0)
-        times_new(1, 0)
-        nc.vector.tensor_tensor(sum_head[:], kept_first[:, 0:head], fresh[0][:, 0:head], ALU.add)
-        times_new(0, 1)
-        nc.vector.tensor_tensor(kept_last[:, cut:S], mem_last[:].indirect(slots(cut, S)), old_all[:, cut:S], ALU.mult)
-        nc.gpsimd.tensor_tensor(sum_tail, kept_first[:, tail:S], fresh[0][:, tail:S], ALU.add)
-        nc.vector.tensor_tensor(sum_mid[:], kept_first[:, head:tail], fresh[0][:, head:tail], ALU.add)
-        times_new(1, 1)
-        nc.vector.tensor_tensor(kept_last[:, 0:cut], picked_last[:], old_half[0][:, 0:cut], ALU.mult)
+        nc.vector.tensor_tensor(fresh0[:, 0:HALF], y0[:, 0:HALF], new_lo, ALU.mult)
+        nc.scalar.activation(picked1, mem1[:].indirect(slots(cut1, S)), ACT.Copy)
+        nc.vector.tensor_tensor(fresh1_lo[:], y1_lo, new_lo, ALU.mult)
+        nc.vector.tensor_tensor(sum_a[:], kept0[:, 0:CUT_A], fresh0[:, 0:CUT_A], ALU.add)
+        nc.scalar.activation(mem0[:].indirect(slots(0, CUT_A)), sum_a[:], ACT.Copy)
 
-        for (lo, hi), source in zip(PIECES, (sum_head[:], sum_mid[:], sum_tail)):
-            nc.scalar.activation(mem_first[:].indirect(slots(lo, hi)), source, ACT.Copy)
-        nc.scalar.dma_start(out[0:P, :], mem_first[:])
-        nc.vector.tensor_tensor(mem_last[:].indirect(slot_sb[:]), kept_last[:], fresh[1][:], ALU.add)
-        nc.sync.dma_start(out[P : 2 * P, :], mem_last[:])
+        nc.vector.tensor_tensor(kept1_lo, mem1[:].indirect(slots(0, HALF)), old_sb[:, 0:HALF], ALU.mult)
+        nc.vector.tensor_tensor(fresh0[:, HALF:S], y0[:, HALF:S], new_hi[:], ALU.mult)
+        tanh_of_product(y1_hi, 1, HALF, S, 7)
+        nc.vector.tensor_tensor(sum1_lo[:], kept1_lo, fresh1_lo[:], ALU.add)
+        nc.vector.tensor_tensor(sum_b[:], kept0[:, CUT_A:CUT_B], fresh0[:, CUT_A:CUT_B], ALU.add)
+        nc.scalar.activation(mem0[:].indirect(slots(CUT_A, CUT_B)), sum_b[:], ACT.Copy)
+        nc.vector.tensor_tensor(kept1_hi[:, 0:fused], mem1[:].indirect(slots(HALF, cut1)), old_sb[:, HALF:cut1], ALU.mult)
+        nc.vector.tensor_tensor(sum_c[:, 0:SPARE], kept0_c[:, 0:SPARE], fresh0[:, CUT_B:mid], ALU.add)
+        nc.vector.tensor_copy(mem1[:].indirect(slots(0, HALF)), sum1_lo[:])
+
+        nc.gpsimd.tensor_tensor(sum_c[:, SPARE : S - CUT_B], kept0_c[:, SPARE : S - CUT_B], fresh0[:, mid:S], ALU.add)
+        nc.gpsimd.tensor_tensor(kept1_hi[:, fused:HALF], picked1, old_sb[:, cut1:S], ALU.mult)
+        nc.gpsimd.tensor_tensor(fresh1_hi, y1_hi, new_hi[:], ALU.mult)
+
+        nc.scalar.activation(mem0[:].indirect(slots(CUT_B, S)), sum_c, ACT.Copy)
+        nc.scalar.dma_start(out[0:P, :], mem0[:])
+        nc.vector.tensor_tensor(mem1[:].indirect(slots(HALF, S)), kept1_hi, fresh1_hi, ALU.add)
+        nc.sync.dma_start(out[P : 2 * P, :], mem1[:])

@@ -81,6 +81,7 @@ def tile_picked_ema_tanh_p_kernel(tc, x_words, x_scales, mem, w1, old, new, offs
         old_sb = keep.tile([P, S], F32, name="old_sb")
         nc.scalar.copy(old_sb[:, 0:HALF], spread(0, 0))
         old_hi = spread(PER_BANK, 1)
+        nc.scalar.copy(old_sb[:, HALF:CUT_B], old_hi[:, 0 : CUT_B - HALF])
         new_lo = spread(CHUNKS, 2)
 
         x_scale = keep.tile([P, S], U8, name="x_scale")
@@ -98,7 +99,7 @@ def tile_picked_ema_tanh_p_kernel(tc, x_words, x_scales, mem, w1, old, new, offs
         w_code = keep.tile([P, N], U32, name="w_code", align_bytes=64)
         w_scale = keep.tile([P, N], U8, name="w_scale", align_bytes=64)
         nc.vector.quantize_mx(out=w_code[:].bitcast(FP8X4), scales=w_scale[:], in_=w_bf[:].rearrange("p n t -> p (n t)"))
-        nc.vector.tensor_copy(old_sb[:, HALF:S], old_hi)
+        nc.vector.tensor_copy(old_sb[:, CUT_B:S], old_hi[:, CUT_B - HALF : HALF])
 
         def tanh_of_product(dst, b, lo, hi, bank):
             z = psum.tile([P, hi - lo], F32, name="z", tag="bank%d" % bank)

@@ -25,8 +25,8 @@ SCALE_ROWS = K // 32
 SCALES_AT = P - SCALE_ROWS
 STRIPE = 16
 CUT_A, CUT_B = 384, 640
-SPARE = 128
-PICK1 = 384
+SPARE = 192
+PICK1 = 416
 
 
 def tile_picked_ema_tanh_p_kernel(tc, x_words, x_scales, mem, w1, old, new, offs, slot, out):
@@ -59,15 +59,15 @@ def tile_picked_ema_tanh_p_kernel(tc, x_words, x_scales, mem, w1, old, new, offs
         nc.sync.dma_start(offs_sb[:], offs)
         nc.sync.dma_start(word_tab[:].bitcast(I32), x_words[0].rearrange("p n t -> p (n t)").bitcast(I32))
         nc.sync.dma_start(rows[0:CHUNKS, :], old[0:1, :].rearrange("a (c n) -> (a c) n", n=P))
-        nc.sync.dma_start(rows[CHUNKS : CHUNKS + PER_BANK, :], new[0:1, 0:HALF].rearrange("a (c n) -> (a c) n", n=P))
+        nc.sync.dma_start(rows[CHUNKS : 2 * CHUNKS, :], new[0:1, :].rearrange("a (c n) -> (a c) n", n=P))
         nc.sync.dma_start(slot_sb[:], slot)
         nc.sync.dma_start(w_raw[:], w1.rearrange("(p t) n -> p t n", t=PACK))
         nc.sync.dma_start(mem0[:], mem[0:P, :])
 
         turned = psum.tile([P, P], F32, name="turned", tag="bank4")
         nc.tensor.transpose(turned[:], rows[:], ident[:])
-        cols = keep.tile([P, CHUNKS + PER_BANK], F32, name="cols")
-        nc.scalar.copy(cols[:], turned[:, 0 : CHUNKS + PER_BANK])
+        cols = keep.tile([P, 2 * CHUNKS], F32, name="cols")
+        nc.scalar.copy(cols[:], turned[:, 0 : 2 * CHUNKS])
 
         w_bf = keep.tile([P, N, PACK], BF16, name="w_bf", tag="rows_then_w", align_bytes=64)
         nc.scalar.copy(w_bf[:].rearrange("p (c i) t -> p c t i", i=4), w_raw[:].rearrange("p t (c i) -> p c t i", i=4))
@@ -78,7 +78,7 @@ def tile_picked_ema_tanh_p_kernel(tc, x_words, x_scales, mem, w1, old, new, offs
                 nc.tensor.transpose(tile[:, i, :], cols[:, first_col + i : first_col + i + 1].to_broadcast([P, P]), ident[:])
             return tile[:].rearrange("p i n -> p (i n)")
 
-        old_sb = keep.tile([P, S], F32, name="old_sb")
+        old_sb = keep.tile([P, S - 32 + CUT_B - CUT_A], F32, name="old_sb")
         nc.scalar.copy(old_sb[:, 0:HALF], spread(0, 0))
         old_hi = spread(PER_BANK, 1)
         nc.scalar.copy(old_sb[:, HALF:CUT_B], old_hi[:, 0 : CUT_B - HALF])
@@ -114,27 +114,27 @@ def tile_picked_ema_tanh_p_kernel(tc, x_words, x_scales, mem, w1, old, new, offs
             )
             nc.scalar.activation(dst, z[:], ACT.Tanh)
 
-        fused = HALF - PICK1
-        cut1 = S - PICK1
-        work = keep.tile([P, S + HALF], F32, name="work")
+        cut1 = HALF + PICK1
+        work = keep.tile([P, S - 32 + HALF], F32, name="work")
         fresh0 = work[:, 0:S]
-        kept1_lo = work[:, S : S + HALF]
-        y1_lo = work[:, S - HALF // 2 : S + HALF // 2]
+        y1_lo = keep.tile([P, HALF], F32, name="y1_lo")[:]
+        kept1_lo = y1_lo
         mid = CUT_B + SPARE
-        fresh1_hi = work[:, mid : mid + HALF]
-        last = keep.tile([P, 2 * (S - CUT_B) - SPARE], F32, name="last")
+        fresh1_hi = work[:, mid - HALF : mid]
+        last = keep.tile([P, S - CUT_B + HALF // 2], F32, name="last")
         sum_c = last[:, 0 : S - CUT_B]
         kept0_c = last[:, S - CUT_B - SPARE : 2 * (S - CUT_B) - SPARE]
         y0 = keep.tile([P, S], F32, name="y0")
         picked1 = y0[:, 0:PICK1]
         y1_hi = y0[:, HALF:S]
         kept0 = keep.tile([P, CUT_B], F32, name="kept0")
-        kept1_hi = work[:, mid - HALF : mid]
+        kept1_hi = work[:, S - 32 : S - 32 + HALF]
         picked0 = keep.tile([P, S - CUT_B], F32, name="picked0", tag="w_then_picked")
         fresh1_lo = keep.tile([P, HALF], F32, name="fresh1_lo")
         sum1_lo = keep.tile([P, HALF], F32, name="sum1_lo")
         sum_a = keep.tile([P, CUT_A], F32, name="sum_a")
-        sum_b = keep.tile([P, CUT_B - CUT_A], F32, name="sum_b")
+        shared = HALF - CUT_A
+        sum_b = old_sb[:, S - 32 : S - 32 + CUT_B - CUT_A]
 
         nc.scalar.activation(picked0[:], mem0[:].indirect(slots(CUT_B, S)), ACT.Copy)
         nc.vector.tensor_tensor(kept0[:, 0:CUT_B], mem0[:].indirect(slots(0, CUT_B)), old_sb[:, 0:CUT_B], ALU.mult)
@@ -146,24 +146,30 @@ def tile_picked_ema_tanh_p_kernel(tc, x_words, x_scales, mem, w1, old, new, offs
         tanh_of_product(y0[:, HALF:S], 0, HALF, S, 6)
 
         nc.vector.tensor_tensor(fresh0[:, 0:HALF], y0[:, 0:HALF], new_lo, ALU.mult)
-        nc.scalar.activation(picked1, mem1[:].indirect(slots(cut1, S)), ACT.Copy)
+        nc.scalar.activation(picked1, mem1[:].indirect(slots(HALF, cut1)), ACT.Copy)
         nc.vector.tensor_tensor(fresh1_lo[:], y1_lo, new_lo, ALU.mult)
+        new_hi_bank = spread(CHUNKS + PER_BANK, 2)
         nc.vector.tensor_tensor(sum_a[:], kept0[:, 0:CUT_A], fresh0[:, 0:CUT_A], ALU.add)
         nc.scalar.activation(mem0[:].indirect(slots(0, CUT_A)), sum_a[:], ACT.Copy)
 
         nc.vector.tensor_tensor(kept1_lo, mem1[:].indirect(slots(0, HALF)), old_sb[:, 0:HALF], ALU.mult)
-        nc.vector.tensor_tensor(fresh0[:, HALF:S], y0[:, HALF:S], new_hi[:], ALU.mult)
-        tanh_of_product(y1_hi, 1, HALF, S, 7)
+        nc.vector.tensor_tensor(kept1_hi[:, PICK1:HALF], mem1[:].indirect(slots(cut1, S)), old_sb[:, cut1:S], ALU.mult)
+        nc.gpsimd.tensor_tensor(sum_b[:, 0:shared], kept0[:, CUT_A:HALF], fresh0[:, CUT_A:HALF], ALU.add)
+        nc.vector.tensor_tensor(fresh0[:, HALF:S], y0[:, HALF:S], new_hi_bank, ALU.mult)
+        quarter = HALF // 2
+        tanh_of_product(y1_hi[:, quarter:HALF], 1, S - quarter, S, 7)
         nc.vector.tensor_tensor(sum1_lo[:], kept1_lo, fresh1_lo[:], ALU.add)
-        nc.vector.tensor_tensor(sum_b[:], kept0[:, CUT_A:CUT_B], fresh0[:, CUT_A:CUT_B], ALU.add)
-        nc.scalar.activation(mem0[:].indirect(slots(CUT_A, CUT_B)), sum_b[:], ACT.Copy)
-        nc.vector.tensor_tensor(kept1_hi[:, 0:fused], mem1[:].indirect(slots(HALF, cut1)), old_sb[:, HALF:cut1], ALU.mult)
+        nc.vector.tensor_tensor(sum_b[:, shared : CUT_B - CUT_A], kept0[:, HALF:CUT_B], fresh0[:, HALF:CUT_B], ALU.add)
+        nc.scalar.activation(mem0[:].indirect(slots(CUT_A, CUT_B)), sum_b, ACT.Copy)
         nc.vector.tensor_tensor(sum_c[:, 0:SPARE], kept0_c[:, 0:SPARE], fresh0[:, CUT_B:mid], ALU.add)
         nc.vector.tensor_copy(mem1[:].indirect(slots(0, HALF)), sum1_lo[:])
 
         nc.gpsimd.tensor_tensor(sum_c[:, SPARE : S - CUT_B], kept0_c[:, SPARE : S - CUT_B], fresh0[:, mid:S], ALU.add)
-        nc.gpsimd.tensor_tensor(kept1_hi[:, fused:HALF], picked1, old_sb[:, cut1:S], ALU.mult)
-        nc.gpsimd.tensor_tensor(fresh1_hi, y1_hi, new_hi[:], ALU.mult)
+        nc.gpsimd.tensor_tensor(fresh1_hi[:, quarter:HALF], y1_hi[:, quarter:HALF], new_hi[:, quarter:HALF], ALU.mult)
+        nc.gpsimd.tensor_tensor(kept1_hi[:, 0:PICK1], picked1, old_sb[:, HALF:cut1], ALU.mult)
+        y1_late = last[:, S - CUT_B : S - CUT_B + quarter]
+        tanh_of_product(y1_late, 1, HALF, S - quarter, 0)
+        nc.gpsimd.tensor_tensor(fresh1_hi[:, 0:quarter], y1_late, new_hi[:, 0:quarter], ALU.mult)
 
         nc.scalar.activation(mem0[:].indirect(slots(CUT_B, S)), sum_c, ACT.Copy)
         nc.scalar.dma_start(out[0:P, :], mem0[:])

@@ -78,7 +78,7 @@ def tile_picked_ema_tanh_p_kernel(tc, x_words, x_scales, mem, w1, old, new, offs
                 nc.tensor.transpose(tile[:, i, :], cols[:, first_col + i : first_col + i + 1].to_broadcast([P, P]), ident[:])
             return tile[:].rearrange("p i n -> p (i n)")
 
-        old_sb = keep.tile([P, S - 32 + CUT_B - CUT_A], F32, name="old_sb")
+        old_sb = keep.tile([P, S], F32, name="old_sb")
         nc.scalar.copy(old_sb[:, 0:HALF], spread(0, 0))
         old_hi = spread(PER_BANK, 1)
         nc.scalar.copy(old_sb[:, HALF:CUT_B], old_hi[:, 0 : CUT_B - HALF])
@@ -121,20 +121,20 @@ def tile_picked_ema_tanh_p_kernel(tc, x_words, x_scales, mem, w1, old, new, offs
         kept1_lo = y1_lo
         mid = CUT_B + SPARE
         fresh1_hi = work[:, mid - HALF : mid]
-        last = keep.tile([P, S - CUT_B + HALF // 2], F32, name="last")
-        sum_c = last[:, 0 : S - CUT_B]
-        kept0_c = last[:, S - CUT_B - SPARE : 2 * (S - CUT_B) - SPARE]
+        last = keep.tile([P, SPARE + HALF // 2], F32, name="last")
+        kept0_c = last[:, 0 : S - CUT_B]
         y0 = keep.tile([P, S], F32, name="y0")
         picked1 = y0[:, 0:PICK1]
         y1_hi = y0[:, HALF:S]
         kept0 = keep.tile([P, CUT_B], F32, name="kept0")
+        sum_c = kept0[:, CUT_B - (S - CUT_B) : CUT_B]
         kept1_hi = work[:, S - 32 : S - 32 + HALF]
         picked0 = keep.tile([P, S - CUT_B], F32, name="picked0", tag="w_then_picked")
         fresh1_lo = keep.tile([P, HALF], F32, name="fresh1_lo")
         sum1_lo = keep.tile([P, HALF], F32, name="sum1_lo")
         sum_a = keep.tile([P, CUT_A], F32, name="sum_a")
         shared = HALF - CUT_A
-        sum_b = old_sb[:, S - 32 : S - 32 + CUT_B - CUT_A]
+        sum_b = old_sb[:, 0 : CUT_B - CUT_A]
 
         nc.scalar.activation(picked0[:], mem0[:].indirect(slots(CUT_B, S)), ACT.Copy)
         nc.vector.tensor_tensor(kept0[:, 0:CUT_B], mem0[:].indirect(slots(0, CUT_B)), old_sb[:, 0:CUT_B], ALU.mult)
@@ -167,7 +167,7 @@ def tile_picked_ema_tanh_p_kernel(tc, x_words, x_scales, mem, w1, old, new, offs
         nc.gpsimd.tensor_tensor(sum_c[:, SPARE : S - CUT_B], kept0_c[:, SPARE : S - CUT_B], fresh0[:, mid:S], ALU.add)
         nc.gpsimd.tensor_tensor(fresh1_hi[:, quarter:HALF], y1_hi[:, quarter:HALF], new_hi[:, quarter:HALF], ALU.mult)
         nc.gpsimd.tensor_tensor(kept1_hi[:, 0:PICK1], picked1, old_sb[:, HALF:cut1], ALU.mult)
-        y1_late = last[:, S - CUT_B : S - CUT_B + quarter]
+        y1_late = last[:, SPARE : SPARE + quarter]
         tanh_of_product(y1_late, 1, HALF, S - quarter, 0)
         nc.gpsimd.tensor_tensor(fresh1_hi[:, 0:quarter], y1_late, new_hi[:, 0:quarter], ALU.mult)
 

@@ -39,7 +39,7 @@ def tile_picked_ema_tanh_p_kernel(tc, x_words, x_scales, mem, w1, old, new, offs
 
         offs_sb = lists.tile([P, S // STRIPE], U16, name="offs_sb")
         slot_sb = lists.tile([P, S // STRIPE], U16, name="slot_sb")
-        scale_tab = laid.tile([P, T], U8, name="scale_tab", offset=T // 2)
+        scale_tab = laid.tile([P, T], U8, name="scale_tab", offset=4 * S - T // 2)
         word_tab = keep.tile([P, T], U32, name="word_tab")
         x_plane = keep.tile([P, S], U8, name="x_plane", align_bytes=64)
         ident = keep.tile([P, P], F32, name="ident")
@@ -78,7 +78,7 @@ def tile_picked_ema_tanh_p_kernel(tc, x_words, x_scales, mem, w1, old, new, offs
                 nc.tensor.transpose(tile[:, i, :], cols[:, first_col + i : first_col + i + 1].to_broadcast([P, P]), ident[:])
             return tile[:].rearrange("p i n -> p (i n)")
 
-        old_sb = keep.tile([P, S], F32, name="old_sb")
+        old_sb = keep.tile([P, CUT_B], F32, name="old_sb")
         nc.scalar.copy(old_sb[:, 0:HALF], spread(0, 0))
         old_hi = spread(PER_BANK, 1)
         nc.scalar.copy(old_sb[:, HALF:CUT_B], old_hi[:, 0 : CUT_B - HALF])
@@ -88,10 +88,10 @@ def tile_picked_ema_tanh_p_kernel(tc, x_words, x_scales, mem, w1, old, new, offs
         nc.vector.tensor_copy(x_scale[:], scale_tab[:].indirect(offs_sb[:]))
         for r in range(4):
             nc.sync.dma_start(x_plane[r:P:32, :].bitcast(I32), x_scale[SCALES_AT + r : P : 4, :].bitcast(I32))
-        mem1 = laid.tile([P, U], F32, name="mem1", offset=T)
+        mem1 = laid.tile([P, U], F32, name="mem1", offset=4 * S)
         nc.sync.dma_start(mem1[:], mem[P : 2 * P, :])
-        new_hi = laid.tile([P, HALF], F32, name="new_hi", offset=0)
-        nc.sync.dma_start(new_hi[:], new[:, HALF:S])
+        upper = laid.tile([P, S], F32, name="upper", offset=0)
+        nc.sync.dma_start(upper[:, HALF:S], new[:, HALF:S])
 
         x_word = keep.tile([P, S], U32, name="x_word", align_bytes=64)
         nc.vector.tensor_copy(x_word[:], word_tab[:].indirect(offs_sb[:]))
@@ -99,7 +99,7 @@ def tile_picked_ema_tanh_p_kernel(tc, x_words, x_scales, mem, w1, old, new, offs
         w_code = keep.tile([P, N], U32, name="w_code", align_bytes=64)
         w_scale = keep.tile([P, N], U8, name="w_scale", align_bytes=64)
         nc.vector.quantize_mx(out=w_code[:].bitcast(FP8X4), scales=w_scale[:], in_=w_bf[:].rearrange("p n t -> p (n t)"))
-        nc.vector.tensor_copy(old_sb[:, CUT_B:S], old_hi[:, CUT_B - HALF : HALF])
+        nc.vector.tensor_copy(upper[:, HALF - PICK1 : HALF], old_hi[:, HALF - PICK1 : HALF])
 
         def tanh_of_product(dst, b, lo, hi, bank):
             z = psum.tile([P, hi - lo], F32, name="z", tag="bank%d" % bank)
@@ -114,21 +114,23 @@ def tile_picked_ema_tanh_p_kernel(tc, x_words, x_scales, mem, w1, old, new, offs
             )
             nc.scalar.activation(dst, z[:], ACT.Tanh)
 
-        cut1 = HALF + PICK1
-        work = keep.tile([P, S - 32 + HALF], F32, name="work")
-        fresh0 = work[:, 0:S]
+        cut1 = S - PICK1
+        fused = HALF - PICK1
+        quarter = HALF // 2
+        lead = HALF + quarter - CUT_B
+        work = keep.tile([P, lead + S], F32, name="work")
+        fresh0 = work[:, lead : lead + S]
         y1_lo = keep.tile([P, HALF], F32, name="y1_lo")[:]
         kept1_lo = y1_lo
         mid = CUT_B + SPARE
-        fresh1_hi = work[:, mid - HALF : mid]
+        fresh1_hi = work[:, HALF:S]
         last = keep.tile([P, SPARE + HALF // 2], F32, name="last")
         kept0_c = last[:, 0 : S - CUT_B]
         y0 = keep.tile([P, S], F32, name="y0")
-        picked1 = y0[:, 0:PICK1]
-        y1_hi = y0[:, HALF:S]
+        picked1 = y0[:, fused:HALF]
         kept0 = keep.tile([P, CUT_B], F32, name="kept0")
         sum_c = kept0[:, CUT_B - (S - CUT_B) : CUT_B]
-        kept1_hi = work[:, S - 32 : S - 32 + HALF]
+        kept1_hi = work[:, 0:HALF]
         picked0 = keep.tile([P, S - CUT_B], F32, name="picked0", tag="w_then_picked")
         fresh1_lo = keep.tile([P, HALF], F32, name="fresh1_lo")
         sum1_lo = keep.tile([P, HALF], F32, name="sum1_lo")
@@ -138,7 +140,7 @@ def tile_picked_ema_tanh_p_kernel(tc, x_words, x_scales, mem, w1, old, new, offs
 
         nc.scalar.activation(picked0[:], mem0[:].indirect(slots(CUT_B, S)), ACT.Copy)
         nc.vector.tensor_tensor(kept0[:, 0:CUT_B], mem0[:].indirect(slots(0, CUT_B)), old_sb[:, 0:CUT_B], ALU.mult)
-        nc.gpsimd.tensor_tensor(kept0_c, picked0[:], old_sb[:, CUT_B:S], ALU.mult)
+        nc.gpsimd.tensor_tensor(kept0_c, picked0[:], upper[:, CUT_B - HALF : HALF], ALU.mult)
 
         tanh_of_product(y0[:, 0 : HALF // 2], 0, 0, HALF // 2, 3)
         tanh_of_product(y0[:, HALF // 2 : HALF], 0, HALF // 2, HALF, 4)
@@ -146,18 +148,17 @@ def tile_picked_ema_tanh_p_kernel(tc, x_words, x_scales, mem, w1, old, new, offs
         tanh_of_product(y0[:, HALF:S], 0, HALF, S, 6)
 
         nc.vector.tensor_tensor(fresh0[:, 0:HALF], y0[:, 0:HALF], new_lo, ALU.mult)
-        nc.scalar.activation(picked1, mem1[:].indirect(slots(HALF, cut1)), ACT.Copy)
+        nc.scalar.activation(picked1, mem1[:].indirect(slots(cut1, S)), ACT.Copy)
         nc.vector.tensor_tensor(fresh1_lo[:], y1_lo, new_lo, ALU.mult)
         new_hi_bank = spread(CHUNKS + PER_BANK, 2)
         nc.vector.tensor_tensor(sum_a[:], kept0[:, 0:CUT_A], fresh0[:, 0:CUT_A], ALU.add)
         nc.scalar.activation(mem0[:].indirect(slots(0, CUT_A)), sum_a[:], ACT.Copy)
 
         nc.vector.tensor_tensor(kept1_lo, mem1[:].indirect(slots(0, HALF)), old_sb[:, 0:HALF], ALU.mult)
-        nc.vector.tensor_tensor(kept1_hi[:, PICK1:HALF], mem1[:].indirect(slots(cut1, S)), old_sb[:, cut1:S], ALU.mult)
+        nc.vector.tensor_tensor(kept1_hi[:, 0:fused], mem1[:].indirect(slots(HALF, cut1)), old_sb[:, HALF:cut1], ALU.mult)
         nc.gpsimd.tensor_tensor(sum_b[:, 0:shared], kept0[:, CUT_A:HALF], fresh0[:, CUT_A:HALF], ALU.add)
         nc.vector.tensor_tensor(fresh0[:, HALF:S], y0[:, HALF:S], new_hi_bank, ALU.mult)
-        quarter = HALF // 2
-        tanh_of_product(y1_hi[:, quarter:HALF], 1, S - quarter, S, 7)
+        tanh_of_product(y0[:, HALF : HALF + quarter], 1, HALF, HALF + quarter, 7)
         nc.vector.tensor_tensor(sum1_lo[:], kept1_lo, fresh1_lo[:], ALU.add)
         nc.vector.tensor_tensor(sum_b[:, shared : CUT_B - CUT_A], kept0[:, HALF:CUT_B], fresh0[:, HALF:CUT_B], ALU.add)
         nc.scalar.activation(mem0[:].indirect(slots(CUT_A, CUT_B)), sum_b, ACT.Copy)
@@ -165,11 +166,11 @@ def tile_picked_ema_tanh_p_kernel(tc, x_words, x_scales, mem, w1, old, new, offs
         nc.vector.tensor_copy(mem1[:].indirect(slots(0, HALF)), sum1_lo[:])
 
         nc.gpsimd.tensor_tensor(sum_c[:, SPARE : S - CUT_B], kept0_c[:, SPARE : S - CUT_B], fresh0[:, mid:S], ALU.add)
-        nc.gpsimd.tensor_tensor(fresh1_hi[:, quarter:HALF], y1_hi[:, quarter:HALF], new_hi[:, quarter:HALF], ALU.mult)
-        nc.gpsimd.tensor_tensor(kept1_hi[:, 0:PICK1], picked1, old_sb[:, HALF:cut1], ALU.mult)
+        both = slice(fused, HALF + quarter)
+        nc.gpsimd.tensor_tensor(work[:, both], y0[:, both], upper[:, both], ALU.mult)
         y1_late = last[:, SPARE : SPARE + quarter]
-        tanh_of_product(y1_late, 1, HALF, S - quarter, 0)
-        nc.gpsimd.tensor_tensor(fresh1_hi[:, 0:quarter], y1_late, new_hi[:, 0:quarter], ALU.mult)
+        tanh_of_product(y1_late, 1, S - quarter, S, 0)
+        nc.gpsimd.tensor_tensor(fresh1_hi[:, quarter:HALF], y1_late, upper[:, S - quarter : S], ALU.mult)
 
         nc.scalar.activation(mem0[:].indirect(slots(CUT_B, S)), sum_c, ACT.Copy)
         nc.scalar.dma_start(out[0:P, :], mem0[:])

@@ -21,12 +21,15 @@ PACK = 4
 CHUNKS = S // P
 PER_BANK = 4
 HALF = PER_BANK * P
+QUARTER = HALF // 2
+STRIPE = 16
 SCALE_ROWS = K // 32
 SCALES_AT = P - SCALE_ROWS
-STRIPE = 16
-CUT_A, CUT_B = 384, 640
+CUT_A, CUT_B = 256, 640
 SPARE = 192
-PICK1 = 416
+PICK1 = 384
+EARLY = 224
+LAP = 32
 
 
 def tile_picked_ema_tanh_p_kernel(tc, x_words, x_scales, mem, w1, old, new, offs, slot, out):
@@ -72,17 +75,21 @@ def tile_picked_ema_tanh_p_kernel(tc, x_words, x_scales, mem, w1, old, new, offs
         w_bf = keep.tile([P, N, PACK], BF16, name="w_bf", tag="rows_then_w", align_bytes=64)
         nc.scalar.copy(w_bf[:].rearrange("p (c i) t -> p c t i", i=4), w_raw[:].rearrange("p t (c i) -> p c t i", i=4))
 
-        def spread(first_col, bank):
-            tile = psum.tile([P, PER_BANK, P], F32, name="spread", tag="bank%d" % bank)
-            for i in range(PER_BANK):
+        def spread(first_col, count, bank):
+            tile = psum.tile([P, count, P], F32, name="spread", tag="bank%d" % bank)
+            for i in range(count):
                 nc.tensor.transpose(tile[:, i, :], cols[:, first_col + i : first_col + i + 1].to_broadcast([P, P]), ident[:])
             return tile[:].rearrange("p i n -> p (i n)")
 
-        old_sb = keep.tile([P, CUT_B], F32, name="old_sb")
-        nc.scalar.copy(old_sb[:, 0:HALF], spread(0, 0))
-        old_hi = spread(PER_BANK, 1)
-        nc.scalar.copy(old_sb[:, HALF:CUT_B], old_hi[:, 0 : CUT_B - HALF])
-        new_lo = spread(CHUNKS, 2)
+        cut1 = S - PICK1
+        fused = cut1 - HALF
+        olds = keep.tile([P, CUT_B + HALF], F32, name="olds")
+        old_sb = olds[:, 0:CUT_B]
+        nc.scalar.copy(old_sb[:, 0:HALF], spread(0, PER_BANK, 0))
+        nc.scalar.copy(old_sb[:, HALF:CUT_B], spread(PER_BANK, 1, 4))
+        old_last = spread(CUT_B // P, CHUNKS - CUT_B // P, 1)
+        new_lo = spread(CHUNKS, PER_BANK, 2)
+        new_hi = spread(CHUNKS + PER_BANK, PER_BANK, 7)
 
         x_scale = keep.tile([P, S], U8, name="x_scale")
         nc.vector.tensor_copy(x_scale[:], scale_tab[:].indirect(offs_sb[:]))
@@ -99,7 +106,7 @@ def tile_picked_ema_tanh_p_kernel(tc, x_words, x_scales, mem, w1, old, new, offs
         w_code = keep.tile([P, N], U32, name="w_code", align_bytes=64)
         w_scale = keep.tile([P, N], U8, name="w_scale", align_bytes=64)
         nc.vector.quantize_mx(out=w_code[:].bitcast(FP8X4), scales=w_scale[:], in_=w_bf[:].rearrange("p n t -> p (n t)"))
-        nc.vector.tensor_copy(upper[:, HALF - PICK1 : HALF], old_hi[:, HALF - PICK1 : HALF])
+        nc.vector.tensor_copy(upper[:, CUT_B - HALF : HALF], old_last)
 
         def tanh_of_product(dst, b, lo, hi, bank):
             z = psum.tile([P, hi - lo], F32, name="z", tag="bank%d" % bank)
@@ -114,63 +121,68 @@ def tile_picked_ema_tanh_p_kernel(tc, x_words, x_scales, mem, w1, old, new, offs
             )
             nc.scalar.activation(dst, z[:], ACT.Tanh)
 
-        cut1 = S - PICK1
-        fused = HALF - PICK1
-        quarter = HALF // 2
-        lead = HALF + quarter - CUT_B
-        work = keep.tile([P, lead + S], F32, name="work")
-        fresh0 = work[:, lead : lead + S]
-        y1_lo = keep.tile([P, HALF], F32, name="y1_lo")[:]
-        kept1_lo = y1_lo
+        piece_c = S - CUT_B
         mid = CUT_B + SPARE
-        fresh1_hi = work[:, HALF:S]
-        last = keep.tile([P, SPARE + HALF // 2], F32, name="last")
-        kept0_c = last[:, 0 : S - CUT_B]
-        y0 = keep.tile([P, S], F32, name="y0")
-        picked1 = y0[:, fused:HALF]
-        kept0 = keep.tile([P, CUT_B], F32, name="kept0")
-        sum_c = kept0[:, CUT_B - (S - CUT_B) : CUT_B]
+        work = keep.tile([P, S], F32, name="work")
         kept1_hi = work[:, 0:HALF]
-        picked0 = keep.tile([P, S - CUT_B], F32, name="picked0", tag="w_then_picked")
-        fresh1_lo = keep.tile([P, HALF], F32, name="fresh1_lo")
+        fresh1_hi = work[:, HALF:S]
+        fresh0_b = work[:, 0:QUARTER]
+        y0_hi = work[:, HALF:S]
+        kept1_lo = work[:, HALF:S]
+        fresh1_lo = olds[:, CUT_B : CUT_B + HALF]
+        sum_c = olds[:, CUT_B - SPARE : CUT_B - SPARE + piece_c]
+        fresh0_a = keep.tile([P, QUARTER], F32, name="fresh0_a")
+        fresh0_hi = keep.tile([P, HALF], F32, name="fresh0_hi")
+
+        first = keep.tile([P, piece_c - LAP + QUARTER], F32, name="first")
+        kept0_c = first[:, 0:piece_c]
+        y0_a = first[:, piece_c - LAP : piece_c - LAP + QUARTER]
+        y1_late = first[:, piece_c - QUARTER : piece_c]
+
+        ys = keep.tile([P, PICK1 + QUARTER], F32, name="ys")
+        picked1 = ys[:, 0:PICK1]
+        y0_b = ys[:, PICK1 - QUARTER : PICK1]
+        y1_third = ys[:, PICK1 : PICK1 + QUARTER]
+
+        y1_lo = keep.tile([P, HALF], F32, name="y1_lo")
+        kept0 = keep.tile([P, CUT_B], F32, name="kept0")
+        picked0 = keep.tile([P, piece_c], F32, name="picked0", tag="w_then_picked")
         sum1_lo = keep.tile([P, HALF], F32, name="sum1_lo")
-        sum_a = keep.tile([P, CUT_A], F32, name="sum_a")
-        shared = HALF - CUT_A
-        sum_b = old_sb[:, 0 : CUT_B - CUT_A]
+        sums0 = keep.tile([P, CUT_B], F32, name="sums0")
 
         nc.scalar.activation(picked0[:], mem0[:].indirect(slots(CUT_B, S)), ACT.Copy)
-        nc.vector.tensor_tensor(kept0[:, 0:CUT_B], mem0[:].indirect(slots(0, CUT_B)), old_sb[:, 0:CUT_B], ALU.mult)
-        nc.gpsimd.tensor_tensor(kept0_c, picked0[:], upper[:, CUT_B - HALF : HALF], ALU.mult)
+        nc.vector.tensor_tensor(kept0[:], mem0[:].indirect(slots(0, CUT_B)), old_sb, ALU.mult)
+        nc.gpsimd.tensor_tensor(kept0_c[:, 0:EARLY], picked0[:, 0:EARLY], upper[:, CUT_B - HALF : CUT_B - HALF + EARLY], ALU.mult)
 
-        tanh_of_product(y0[:, 0 : HALF // 2], 0, 0, HALF // 2, 3)
-        tanh_of_product(y0[:, HALF // 2 : HALF], 0, HALF // 2, HALF, 4)
-        tanh_of_product(y1_lo, 1, 0, HALF, 5)
-        tanh_of_product(y0[:, HALF:S], 0, HALF, S, 6)
+        tanh_of_product(y0_a, 0, 0, QUARTER, 3)
+        tanh_of_product(y0_b, 0, QUARTER, HALF, 4)
+        tanh_of_product(y0_hi, 0, HALF, S, 6)
+        tanh_of_product(y1_lo[:], 1, 0, HALF, 5)
+        tanh_of_product(y1_third, 1, HALF, HALF + QUARTER, 0)
 
-        nc.vector.tensor_tensor(fresh0[:, 0:HALF], y0[:, 0:HALF], new_lo, ALU.mult)
+        nc.vector.tensor_tensor(fresh0_a[:], y0_a, new_lo[:, 0:QUARTER], ALU.mult)
+        nc.gpsimd.tensor_tensor(sums0[:, 0:QUARTER], kept0[:, 0:QUARTER], fresh0_a[:], ALU.add)
+        nc.vector.tensor_tensor(kept0_c[:, EARLY:piece_c], picked0[:, EARLY:piece_c], old_last[:, EARLY:piece_c], ALU.mult)
+        nc.vector.tensor_tensor(fresh0_b, y0_b, new_lo[:, QUARTER:HALF], ALU.mult)
+        nc.gpsimd.tensor_tensor(sums0[:, QUARTER:HALF], kept0[:, QUARTER:HALF], fresh0_b, ALU.add)
         nc.scalar.activation(picked1, mem1[:].indirect(slots(cut1, S)), ACT.Copy)
-        nc.vector.tensor_tensor(fresh1_lo[:], y1_lo, new_lo, ALU.mult)
-        new_hi_bank = spread(CHUNKS + PER_BANK, 2)
-        nc.vector.tensor_tensor(sum_a[:], kept0[:, 0:CUT_A], fresh0[:, 0:CUT_A], ALU.add)
-        nc.scalar.activation(mem0[:].indirect(slots(0, CUT_A)), sum_a[:], ACT.Copy)
+        nc.vector.tensor_tensor(fresh0_hi[:], y0_hi, new_hi, ALU.mult)
+        nc.vector.tensor_tensor(fresh1_lo, y1_lo[:], new_lo, ALU.mult)
+        nc.scalar.activation(mem0[:].indirect(slots(0, CUT_A)), sums0[:, 0:CUT_A], ACT.Copy)
 
         nc.vector.tensor_tensor(kept1_lo, mem1[:].indirect(slots(0, HALF)), old_sb[:, 0:HALF], ALU.mult)
+        nc.vector.tensor_tensor(sums0[:, HALF:CUT_B], kept0[:, HALF:CUT_B], fresh0_hi[:, 0 : CUT_B - HALF], ALU.add)
+        nc.scalar.activation(mem0[:].indirect(slots(CUT_A, CUT_B)), sums0[:, CUT_A:CUT_B], ACT.Copy)
         nc.vector.tensor_tensor(kept1_hi[:, 0:fused], mem1[:].indirect(slots(HALF, cut1)), old_sb[:, HALF:cut1], ALU.mult)
-        nc.gpsimd.tensor_tensor(sum_b[:, 0:shared], kept0[:, CUT_A:HALF], fresh0[:, CUT_A:HALF], ALU.add)
-        nc.vector.tensor_tensor(fresh0[:, HALF:S], y0[:, HALF:S], new_hi_bank, ALU.mult)
-        tanh_of_product(y0[:, HALF : HALF + quarter], 1, HALF, HALF + quarter, 7)
-        nc.vector.tensor_tensor(sum1_lo[:], kept1_lo, fresh1_lo[:], ALU.add)
-        nc.vector.tensor_tensor(sum_b[:, shared : CUT_B - CUT_A], kept0[:, HALF:CUT_B], fresh0[:, HALF:CUT_B], ALU.add)
-        nc.scalar.activation(mem0[:].indirect(slots(CUT_A, CUT_B)), sum_b, ACT.Copy)
-        nc.vector.tensor_tensor(sum_c[:, 0:SPARE], kept0_c[:, 0:SPARE], fresh0[:, CUT_B:mid], ALU.add)
+        nc.vector.tensor_tensor(sum1_lo[:], kept1_lo, fresh1_lo, ALU.add)
+        nc.vector.tensor_tensor(sum_c[:, 0:SPARE], kept0_c[:, 0:SPARE], fresh0_hi[:, CUT_B - HALF : mid - HALF], ALU.add)
         nc.vector.tensor_copy(mem1[:].indirect(slots(0, HALF)), sum1_lo[:])
 
-        nc.gpsimd.tensor_tensor(sum_c[:, SPARE : S - CUT_B], kept0_c[:, SPARE : S - CUT_B], fresh0[:, mid:S], ALU.add)
-        both = slice(fused, HALF + quarter)
-        nc.gpsimd.tensor_tensor(work[:, both], y0[:, both], upper[:, both], ALU.mult)
-        y1_late = last[:, SPARE : SPARE + quarter]
-        tanh_of_product(y1_late, 1, S - quarter, S, 0)
-        nc.gpsimd.tensor_tensor(fresh1_hi[:, quarter:HALF], y1_late, upper[:, S - quarter : S], ALU.mult)
+        nc.gpsimd.tensor_tensor(sum_c[:, SPARE:piece_c], kept0_c[:, SPARE:piece_c], fresh0_hi[:, mid - HALF : HALF], ALU.add)
+        both = slice(fused, HALF + QUARTER)
+        nc.gpsimd.tensor_tensor(work[:, both], ys[:], upper[:, both], ALU.mult)
+        tanh_of_product(y1_late, 1, S - QUARTER, S, 3)
+        nc.gpsimd.tensor_tensor(fresh1_hi[:, QUARTER:HALF], y1_late, upper[:, S - QUARTER : S], ALU.mult)
 
         nc.scalar.activation(mem0[:].indirect(slots(CUT_B, S)), sum_c, ACT.Copy)
         nc.scalar.dma_start(out[0:P, :], mem0[:])

@@ -27,7 +27,7 @@ SCALE_ROWS = K // 32
 SCALES_AT = P - SCALE_ROWS
 CUT_A, CUT_B = 256, 640
 SPARE = 192
-PICK1 = 384
+PICK1 = 448
 EARLY = 224
 LAP = 32
 
@@ -86,7 +86,8 @@ def tile_picked_ema_tanh_p_kernel(tc, x_words, x_scales, mem, w1, old, new, offs
         olds = keep.tile([P, CUT_B + HALF], F32, name="olds")
         old_sb = olds[:, 0:CUT_B]
         nc.scalar.copy(old_sb[:, 0:HALF], spread(0, PER_BANK, 0))
-        nc.scalar.copy(old_sb[:, HALF:CUT_B], spread(PER_BANK, 1, 4))
+        old_fifth = spread(PER_BANK, 1, 4)
+        nc.scalar.copy(old_sb[:, HALF:CUT_B], old_fifth)
         old_last = spread(CUT_B // P, CHUNKS - CUT_B // P, 1)
         new_lo = spread(CHUNKS, PER_BANK, 2)
         new_hi = spread(CHUNKS + PER_BANK, PER_BANK, 7)
@@ -107,6 +108,7 @@ def tile_picked_ema_tanh_p_kernel(tc, x_words, x_scales, mem, w1, old, new, offs
         w_scale = keep.tile([P, N], U8, name="w_scale", align_bytes=64)
         nc.vector.quantize_mx(out=w_code[:].bitcast(FP8X4), scales=w_scale[:], in_=w_bf[:].rearrange("p n t -> p (n t)"))
         nc.vector.tensor_copy(upper[:, CUT_B - HALF : HALF], old_last)
+        nc.scalar.copy(upper[:, fused : CUT_B - HALF], old_fifth[:, fused:P])
 
         def tanh_of_product(dst, b, lo, hi, bank):
             z = psum.tile([P, hi - lo], F32, name="z", tag="bank%d" % bank)

from contextlib import ExitStack

import concourse.mybir as mybir
from concourse.masks import make_identity

K, T, S, N, U = 512, 2048, 1024, 256, 2048
FLOPS = 2 * K * S * N

F32 = mybir.dt.float32
BF16 = mybir.dt.bfloat16
I32 = mybir.dt.int32
U32 = mybir.dt.uint32
U16 = mybir.dt.uint16
U8 = mybir.dt.uint8
FP8X4 = mybir.dt.float8_e4m3fn_x4
ACT = mybir.ActivationFunctionType
ALU = mybir.AluOpType

P = 128
PACK = 4
CHUNKS = S // P
PER_BANK = 4
HALF = PER_BANK * P
QUARTER = HALF // 2
STRIPE = 16
SCALE_ROWS = K // 32
SCALES_AT = P - SCALE_ROWS
CUT_A, CUT_B = 256, 640
SPARE = 192
PICK1 = 448
EARLY = 224
LAP = 32


def tile_picked_ema_tanh_p_kernel(tc, x_words, x_scales, mem, w1, old, new, offs, slot, out):
    nc = tc.nc
    with ExitStack() as ctx:
        lists = ctx.enter_context(tc.tile_pool(name="lists", bufs=1))
        keep = ctx.enter_context(tc.tile_pool(name="keep", bufs=1))
        laid = ctx.enter_context(tc.tile_pool(name="laid", bufs=1))
        psum = ctx.enter_context(tc.psum_pool(name="psum", bufs=1))

        offs_sb = lists.tile([P, S // STRIPE], U16, name="offs_sb")
        slot_sb = lists.tile([P, S // STRIPE], U16, name="slot_sb")
        scale_tab = laid.tile([P, T], U8, name="scale_tab", offset=4 * S - T // 2)
        word_tab = keep.tile([P, T], U32, name="word_tab")
        x_plane = keep.tile([P, S], U8, name="x_plane", align_bytes=64)
        ident = keep.tile([P, P], F32, name="ident")
        rows = keep.tile([P, P], F32, name="rows", tag="rows_then_w", align_bytes=64)
        w_raw = keep.tile([P, PACK, N], F32, name="w_raw", tag="w_then_picked")
        mem0 = keep.tile([P, U], F32, name="mem0")

        def slots(lo, hi):
            return slot_sb[:, lo // STRIPE : hi // STRIPE]

        nc.gpsimd.memset(rows[:], 0.0)
        nc.vector.memset(scale_tab[0:SCALES_AT, :].bitcast(I32), 0)
        make_identity(nc, ident[:])
        nc.vector.memset(x_plane[:].bitcast(I32), 0)

        nc.scalar.dma_start(scale_tab[SCALES_AT:P, :].bitcast(I32), x_scales[0].bitcast(I32))
        nc.sync.dma_start(offs_sb[:], offs)
        nc.sync.dma_start(word_tab[:].bitcast(I32), x_words[0].rearrange("p n t -> p (n t)").bitcast(I32))
        nc.sync.dma_start(rows[0:CHUNKS, :], old[0:1, :].rearrange("a (c n) -> (a c) n", n=P))
        nc.sync.dma_start(rows[CHUNKS : 2 * CHUNKS, :], new[0:1, :].rearrange("a (c n) -> (a c) n", n=P))
        nc.sync.dma_start(slot_sb[:], slot)
        nc.sync.dma_start(w_raw[:], w1.rearrange("(p t) n -> p t n", t=PACK))
        nc.sync.dma_start(mem0[:], mem[0:P, :])

        turned = psum.tile([P, P], F32, name="turned", tag="bank4")
        nc.tensor.transpose(turned[:], rows[:], ident[:])
        cols = keep.tile([P, 2 * CHUNKS], F32, name="cols")
        nc.scalar.copy(cols[:], turned[:, 0 : 2 * CHUNKS])

        w_bf = keep.tile([P, N, PACK], BF16, name="w_bf", tag="rows_then_w", align_bytes=64)
        nc.scalar.copy(w_bf[:].rearrange("p (c i) t -> p c t i", i=4), w_raw[:].rearrange("p t (c i) -> p c t i", i=4))

        def spread(first_col, count, bank):
            tile = psum.tile([P, count, P], F32, name="spread", tag="bank%d" % bank)
            for i in range(count):
                nc.tensor.transpose(tile[:, i, :], cols[:, first_col + i : first_col + i + 1].to_broadcast([P, P]), ident[:])
            return tile[:].rearrange("p i n -> p (i n)")

        cut1 = S - PICK1
        fused = cut1 - HALF
        olds = keep.tile([P, CUT_B + HALF], F32, name="olds")
        old_sb = olds[:, 0:CUT_B]
        nc.scalar.copy(old_sb[:, 0:HALF], spread(0, PER_BANK, 0))
        old_fifth = spread(PER_BANK, 1, 4)
        nc.scalar.copy(old_sb[:, HALF:CUT_B], old_fifth)
        old_last = spread(CUT_B // P, CHUNKS - CUT_B // P, 1)
        new_lo = spread(CHUNKS, PER_BANK, 2)
        new_hi = spread(CHUNKS + PER_BANK, PER_BANK, 7)

        x_scale = keep.tile([P, S], U8, name="x_scale")
        nc.vector.tensor_copy(x_scale[:], scale_tab[:].indirect(offs_sb[:]))
        for r in range(4):
            nc.sync.dma_start(x_plane[r:P:32, :].bitcast(I32), x_scale[SCALES_AT + r : P : 4, :].bitcast(I32))
        mem1 = laid.tile([P, U], F32, name="mem1", offset=4 * S)
        nc.sync.dma_start(mem1[:], mem[P : 2 * P, :])
        upper = laid.tile([P, S], F32, name="upper", offset=0)
        nc.sync.dma_start(upper[:, HALF:S], new[:, HALF:S])

        x_word = keep.tile([P, S], U32, name="x_word", align_bytes=64)
        nc.vector.tensor_copy(x_word[:], word_tab[:].indirect(offs_sb[:]))

        w_code = keep.tile([P, N], U32, name="w_code", align_bytes=64)
        w_scale = keep.tile([P, N], U8, name="w_scale", align_bytes=64)
        nc.vector.quantize_mx(out=w_code[:].bitcast(FP8X4), scales=w_scale[:], in_=w_bf[:].rearrange("p n t -> p (n t)"))
        nc.vector.tensor_copy(upper[:, CUT_B - HALF : HALF], old_last)
        nc.scalar.copy(upper[:, fused : CUT_B - HALF], old_fifth[:, fused:P])

        def tanh_of_product(dst, b, lo, hi, bank):
            z = psum.tile([P, hi - lo], F32, name="z", tag="bank%d" % bank)
            nc.tensor.matmul_mx(
                out=z[:],
                lhsT=w_code[:, b * P : (b + 1) * P].bitcast(FP8X4),
                lhsT_scale=w_scale[:, b * P : (b + 1) * P],
                rhs=x_word[:, lo:hi].bitcast(FP8X4),
                rhs_scale=x_plane[:, lo:hi],
                start=True,
                stop=True,
            )
            nc.scalar.activation(dst, z[:], ACT.Tanh)

        piece_c = S - CUT_B
        mid = CUT_B + SPARE
        work = keep.tile([P, S], F32, name="work")
        kept1_hi = work[:, 0:HALF]
        fresh1_hi = work[:, HALF:S]
        fresh0_b = work[:, 0:QUARTER]
        y0_hi = work[:, HALF:S]
        kept1_lo = work[:, HALF:S]
        fresh1_lo = olds[:, CUT_B : CUT_B + HALF]
        sum_c = olds[:, CUT_B - SPARE : CUT_B - SPARE + piece_c]
        fresh0_a = keep.tile([P, QUARTER], F32, name="fresh0_a")
        fresh0_hi = keep.tile([P, HALF], F32, name="fresh0_hi")

        first = keep.tile([P, piece_c - LAP + QUARTER], F32, name="first")
        kept0_c = first[:, 0:piece_c]
        y0_a = first[:, piece_c - LAP : piece_c - LAP + QUARTER]
        y1_late = first[:, piece_c - QUARTER : piece_c]

        ys = keep.tile([P, PICK1 + QUARTER], F32, name="ys")
        picked1 = ys[:, 0:PICK1]
        y0_b = ys[:, PICK1 - QUARTER : PICK1]
        y1_third = ys[:, PICK1 : PICK1 + QUARTER]

        y1_lo = keep.tile([P, HALF], F32, name="y1_lo")
        kept0 = keep.tile([P, CUT_B], F32, name="kept0")
        picked0 = keep.tile([P, piece_c], F32, name="picked0", tag="w_then_picked")
        sum1_lo = keep.tile([P, HALF], F32, name="sum1_lo")
        sums0 = keep.tile([P, CUT_B], F32, name="sums0")

        nc.scalar.activation(picked0[:], mem0[:].indirect(slots(CUT_B, S)), ACT.Copy)
        nc.vector.tensor_tensor(kept0[:], mem0[:].indirect(slots(0, CUT_B)), old_sb, ALU.mult)
        nc.gpsimd.tensor_tensor(kept0_c[:, 0:EARLY], picked0[:, 0:EARLY], upper[:, CUT_B - HALF : CUT_B - HALF + EARLY], ALU.mult)

        tanh_of_product(y0_a, 0, 0, QUARTER, 3)
        tanh_of_product(y0_b, 0, QUARTER, HALF, 4)
        tanh_of_product(y0_hi, 0, HALF, S, 6)
        tanh_of_product(y1_lo[:], 1, 0, HALF, 5)
        tanh_of_product(y1_third, 1, HALF, HALF + QUARTER, 0)

        nc.vector.tensor_tensor(fresh0_a[:], y0_a, new_lo[:, 0:QUARTER], ALU.mult)
        nc.gpsimd.tensor_tensor(sums0[:, 0:QUARTER], kept0[:, 0:QUARTER], fresh0_a[:], ALU.add)
        nc.vector.tensor_tensor(kept0_c[:, EARLY:piece_c], picked0[:, EARLY:piece_c], old_last[:, EARLY:piece_c], ALU.mult)
        nc.vector.tensor_tensor(fresh0_b, y0_b, new_lo[:, QUARTER:HALF], ALU.mult)
        nc.gpsimd.tensor_tensor(sums0[:, QUARTER:HALF], kept0[:, QUARTER:HALF], fresh0_b, ALU.add)
        nc.scalar.activation(picked1, mem1[:].indirect(slots(cut1, S)), ACT.Copy)
        nc.vector.tensor_tensor(fresh0_hi[:], y0_hi, new_hi, ALU.mult)
        nc.vector.tensor_tensor(fresh1_lo, y1_lo[:], new_lo, ALU.mult)
        nc.scalar.activation(mem0[:].indirect(slots(0, CUT_A)), sums0[:, 0:CUT_A], ACT.Copy)

        nc.vector.tensor_tensor(kept1_lo, mem1[:].indirect(slots(0, HALF)), old_sb[:, 0:HALF], ALU.mult)
        nc.vector.tensor_tensor(sums0[:, HALF:CUT_B], kept0[:, HALF:CUT_B], fresh0_hi[:, 0 : CUT_B - HALF], ALU.add)
        nc.scalar.activation(mem0[:].indirect(slots(CUT_A, CUT_B)), sums0[:, CUT_A:CUT_B], ACT.Copy)
        nc.vector.tensor_tensor(kept1_hi[:, 0:fused], mem1[:].indirect(slots(HALF, cut1)), old_sb[:, HALF:cut1], ALU.mult)
        nc.vector.tensor_tensor(sum1_lo[:], kept1_lo, fresh1_lo, ALU.add)
        nc.vector.tensor_tensor(sum_c[:, 0:SPARE], kept0_c[:, 0:SPARE], fresh0_hi[:, CUT_B - HALF : mid - HALF], ALU.add)
        nc.vector.tensor_copy(mem1[:].indirect(slots(0, HALF)), sum1_lo[:])

        nc.gpsimd.tensor_tensor(sum_c[:, SPARE:piece_c], kept0_c[:, SPARE:piece_c], fresh0_hi[:, mid - HALF : HALF], ALU.add)
        both = slice(fused, HALF + QUARTER)
        nc.gpsimd.tensor_tensor(work[:, both], ys[:], upper[:, both], ALU.mult)
        tanh_of_product(y1_late, 1, S - QUARTER, S, 3)
        nc.gpsimd.tensor_tensor(fresh1_hi[:, QUARTER:HALF], y1_late, upper[:, S - QUARTER : S], ALU.mult)

        nc.scalar.activation(mem0[:].indirect(slots(CUT_B, S)), sum_c, ACT.Copy)
        nc.scalar.dma_start(out[0:P, :], mem0[:])
        nc.vector.tensor_tensor(mem1[:].indirect(slots(HALF, S)), kept1_hi, fresh1_hi, ALU.add)
        nc.sync.dma_start(out[P : 2 * P, :], mem1[:])
